import numpy as np
import ml_dtypes


def mxq(x, axis, fmt="e4m3"):
    dtype, down = {"e4m3": (ml_dtypes.float8_e4m3fn, 7), "e5m2": (ml_dtypes.float8_e5m2, 14)}[fmt]
    v = np.moveaxis(np.asarray(x, np.float32).astype(ml_dtypes.bfloat16).astype(np.float64), axis, -1)
    blocks = v.reshape(v.shape[:-1] + (-1, 32))
    amax = np.abs(blocks).max(-1, keepdims=True)
    byte = np.maximum(np.where(amax > 0, np.frexp(amax)[1] - 1 + 127, 0) - down, 1)
    scale = np.exp2(byte - 127.0)
    codes = (blocks / scale).astype(np.float32).astype(dtype).astype(np.float64)
    return np.moveaxis((codes * scale).reshape(v.shape), -1, axis)


WIDE = False


def mx_kscale(k):
    if not WIDE:
        return np.ones(k)
    levels = np.array([24, -24, 12, -12, 0])
    if k % 512:
        return np.exp2(np.random.permutation(np.resize(levels, k // 32))).repeat(32)
    a = np.empty((k // 512, 16))
    for p in range(k // 512):
        a[p, :8] = np.random.permutation(np.resize(levels, 8))
        for g in range(8):
            far = levels[np.abs(levels - a[p, g]) >= 10]
            a[p, g + 8] = far[np.random.randint(len(far))]
    return np.exp2(a.ravel()).repeat(32)


def f64(x):
    return np.asarray(x).astype(np.float64)


def striped(idx):
    return np.tile(idx.reshape(-1, 16).T, (8, 1)).astype(np.uint16)


def unstriped(offs):
    return offs[:16].T.reshape(-1).astype(np.int64)


E2M1 = np.array([0.0, 0.5, 1.0, 1.5, 2.0, 3.0, 4.0, 6.0, -0.0, -0.5, -1.0, -1.5, -2.0, -3.0, -4.0, -6.0])


def pack_weight(w, fmt):
    k, n = w.shape
    w = f64(np.asarray(w, np.float32).astype(ml_dtypes.bfloat16)).reshape(k // 32, 32, n)
    amax = np.abs(w).max(1)
    if fmt == "e4m3":
        byte = np.frexp(amax)[1] - 1 + 127 - 7
    else:
        mant, ex = np.frexp(amax / 6.0)
        byte = np.where(mant > 0.5, ex, ex - 1) + 127
    byte = np.clip(np.where(amax > 0, byte, 1), 1, 254)
    scaled = (w * np.exp2(127.0 - byte)[:, None, :]).reshape(k, n).astype(np.float32)
    by_word = np.ascontiguousarray(scaled.reshape(k // 512, 128, 4, n).transpose(0, 1, 3, 2))
    if fmt == "e4m3":
        words = by_word.astype(ml_dtypes.float8_e4m3fn).view(np.uint8)
    else:
        c = by_word.astype(ml_dtypes.float4_e2m1fn).view(np.uint8) & 0xF
        words = (c[..., 0::2] | (c[..., 1::2] << 4)).reshape(k // 512, 128, 2 * n)
    return np.ascontiguousarray(words), np.ascontiguousarray(byte.astype(np.uint8).reshape(k // 512, 16, n))


def unpack_weight(words, scales, fmt):
    g, _, n = scales.shape
    words = np.ascontiguousarray(words).reshape(g, 128, n, -1)
    if fmt == "e4m3":
        vals = words.view(ml_dtypes.float8_e4m3fn).astype(np.float64)
    else:
        nib = np.empty((g, 128, n, 4), np.uint8)
        nib[..., 0::2] = words & 0xF
        nib[..., 1::2] = words >> 4
        vals = E2M1[nib]
    vals = vals * np.repeat(np.exp2(scales.astype(np.float64) - 127.0), 8, axis=1)[..., None]
    return vals.transpose(0, 1, 3, 2).reshape(g * 512, n)


def pack_table4(v):
    words, scales = pack_weight(v, "e2m1")
    g, t = words.shape[0] // 2, v.shape[1]
    return np.ascontiguousarray(words.reshape(g, 2, 128, t, 2).transpose(0, 2, 3, 1, 4).reshape(g, 128, t, 4)), scales


def unpack_table4(words, scales):
    g, _, t, _ = words.shape
    return unpack_weight(words.reshape(g, 128, t, 2, 2).transpose(0, 3, 1, 2, 4).reshape(2 * g, 128, 2 * t), scales, "e2m1")


def silu(f):
    return f / (1.0 + np.exp(-np.maximum(f, -700.0)))


def sigm(f):
    return 1.0 / (1.0 + np.exp(-np.maximum(f, -700.0)))


K, N, T, J = 1024, 512, 2048, 1024


def setup_inputs():
    n = np.random.standard_normal
    s = mx_kscale(K)[:, None]
    p_tab = pack_table4(n((K, T)) * s)
    p_wa = pack_weight(n((K, N)) / np.sqrt(2 * K) / s, "e4m3")
    p_wb = pack_weight(n((K, N)) / np.sqrt(2 * K) / s, "e2m1")
    p_wc = pack_weight(n((K, N)) / np.sqrt(K) / s, "e2m1")
    return {
        "tab_words": p_tab[0],
        "tab_scales": p_tab[1],
        "wa_words": p_wa[0],
        "wa_scales": p_wa[1],
        "wb_words": p_wb[0],
        "wb_scales": p_wb[1],
        "wc_words": p_wc[0],
        "wc_scales": p_wc[1],
        "wo": (n((K, N)) / np.sqrt(K) / s).astype(np.float32),
        "b": (0.3 * n(N)).astype(np.float32),
        "wgo": np.tile(np.random.uniform(0.5, 2.0, J), (128, 1)).astype(np.float32),
        "offs": striped(np.random.permutation(T)[:J]),
        "offs2": striped(np.random.permutation(T)[:J]),
    }


def reference(tab_words, tab_scales, wa_words, wa_scales, wb_words, wb_scales, wc_words, wc_scales, wo, b, wgo, offs, offs2):
    idx = unstriped(offs)
    idx2 = unstriped(offs2)
    tab_ = unpack_table4(tab_words, tab_scales)[:, idx]
    tabb_ = unpack_table4(tab_words, tab_scales)[:, idx2]
    wa_ = unpack_weight(wa_words, wa_scales, "e4m3")
    wb_ = unpack_weight(wb_words, wb_scales, "e2m1")
    za = wa_.T @ tabb_ + wb_.T @ tab_
    eta = sigm(za)
    wc_ = unpack_weight(wc_words, wc_scales, "e2m1")
    ms = wc_.T @ tab_
    wo_ = mxq(f64(wo), 0, "e4m3")
    ow = wo_.T @ tabb_
    out = np.zeros((N, T))
    out[:, idx2] = f64(wgo)[0] * (silu(ow + eta * ms + f64(b)[:, None]))
    return out

@@ -1,0 +1,223 @@
+from contextlib import ExitStack
+
+import concourse.mybir as mybir
+
+K, N, T, J = 1024, 512, 2048, 1024
+FLOPS = 4 * 2 * K * N * J
+
+F32 = mybir.dt.float32
+BF16 = mybir.dt.bfloat16
+I32 = mybir.dt.int32
+U32 = mybir.dt.uint32
+U16 = mybir.dt.uint16
+U8 = mybir.dt.uint8
+FP8X4 = mybir.dt.float8_e4m3fn_x4
+FP4X4 = mybir.dt.float4_e2m1fn_x4
+ACT = mybir.ActivationFunctionType
+ALU = mybir.AluOpType
+
+P = 128
+PASSES = 2
+JH = 512
+HALVES = J // JH
+NT = N // P
+NH = 256
+SHIFT_ROWS = 112
+
+
+def tile_list_rgg_ownsilu_kernel(
+    tc, tab_words, tab_scales, wa_words, wa_scales, wb_words, wb_scales, wc_words, wc_scales, wo, b, wgo, offs, offs2, out
+):
+    nc = tc.nc
+    with ExitStack() as ctx:
+        keep = ctx.enter_context(tc.tile_pool(name="keep", bufs=1))
+        work = ctx.enter_context(tc.tile_pool(name="work", bufs=3))
+        psum = ctx.enter_context(tc.psum_pool(name="psum", bufs=1))
+
+        src_list = keep.tile([P, J // 16], U16, name="src_list")
+        dst_list = keep.tile([P, J // 16], U16, name="dst_list")
+        lists = (dst_list, src_list)
+        DST, SRC = 0, 1
+
+        tab_w = keep.tile([P, T], I32, name="tab_w", align_bytes=64)
+        tab_s = keep.tile([P, T // 4], I32, name="tab_s", align_bytes=64)
+        w_s = keep.tile([P, 3 * PASSES * N // 4], I32, name="w_s", align_bytes=64)
+        shifted = keep.tile([P, HALVES * 2 * JH // 4 + 1], I32, name="shifted", align_bytes=64)
+        windows = [keep.tile([P, T], F32, name=f"window{i}", align_bytes=64) for i in range(2)]
+        warm = keep.tile([P, 1], F32, name="warm")
+        bias = keep.tile([P, NT], F32, name="bias")
+
+        nc.gpsimd.memset(tab_s[:], 0)
+        nc.gpsimd.memset(w_s[:], 0)
+        for window in windows:
+            nc.gpsimd.memset(window[:], 0.0)
+        nc.vector.memset(warm[:], 0.0)
+        nc.vector.memset(shifted[:], 0)
+        nc.scalar.activation(warm[:], warm[:], ACT.Silu)
+
+        nc.sync.dma_start(dst_list[:], offs2)
+        nc.sync.dma_start(src_list[:], offs)
+        for r in range(4):
+            nc.sync.dma_start(
+                tab_s[r:P:16, :], tab_scales.bitcast(I32).rearrange("a (q r) t -> r q a t", r=4)[r]
+            )
+        nc.sync.dma_start(tab_w[:], tab_words[0].rearrange("p t b -> p (t b)").bitcast(I32))
+        row_words = PASSES * N // 4
+        w_rows = keep.tile([16, 3 * row_words], I32, name="w_rows")
+        for w, scales in enumerate((wa_scales, wb_scales, wc_scales)):
+            nc.sync.dma_start(
+                w_rows[:, w * row_words : (w + 1) * row_words].rearrange("q (a n) -> q a n", a=PASSES),
+                scales.bitcast(I32).rearrange("a q n -> q a n"),
+            )
+        w_s8 = w_s[:].bitcast(U8)
+
+        wo_raw = {}
+
+        def load_wo(g):
+            wo_raw[g] = [keep.tile([P, 4, NH], F32, name=f"wo_raw{a}") for a in range(PASSES)]
+            for a in range(PASSES):
+                rows = wo[512 * a : 512 * (a + 1), g * NH : (g + 1) * NH]
+                nc.sync.dma_start(wo_raw[g][a][:], rows.rearrange("(p i) n -> p i n", i=4))
+
+        wa_w = keep.tile([P, PASSES, N], I32, name="wa_w", align_bytes=64)
+        wb_w = keep.tile([P, PASSES, N // 2], I32, name="wb_w", align_bytes=64)
+        wc_w = keep.tile([P, PASSES, N // 2], I32, name="wc_w", align_bytes=64)
+        load_wo(0)
+        for q in range(4):
+            nc.sync.dma_start(w_s[32 * q : 32 * q + 4, :], w_rows[4 * q : 4 * q + 4, :])
+        nc.sync.dma_start(wa_w[:], wa_words.rearrange("a p n i -> p a (n i)").bitcast(I32))
+        nc.sync.dma_start(wb_w[:], wb_words.rearrange("a p x -> p a x").bitcast(I32))
+        nc.sync.dma_start(wc_w[:], wc_words.rearrange("a p x -> p a x").bitcast(I32))
+        with nc.allow_non_contiguous_dma(reason="one bias value for each partition and row tile"):
+            nc.sync.dma_start(bias[:], b.rearrange("(c p) -> p c", p=P))
+
+        wo_bf = [keep.tile([P, PASSES, NH * 4], BF16, name=f"wo_bf{g}", align_bytes=64) for g in range(N // NH)]
+        wo_w = [keep.tile([P, PASSES, NH], U32, name=f"wo_w{g}", align_bytes=64) for g in range(N // NH)]
+        wo_s = [keep.tile([P, PASSES, NH], U8, name=f"wo_s{g}", align_bytes=64) for g in range(N // NH)]
+
+        def cast_wo(g):
+            for a in range(PASSES):
+                nc.scalar.activation(
+                    wo_bf[g][:, a, :].rearrange("p (c e i) -> p c i e", e=4, i=4),
+                    wo_raw[g][a][:].rearrange("p i (c e) -> p c i e", e=4),
+                    ACT.Copy,
+                )
+
+        def quantize_wo(g):
+            nc.vector.quantize_mx(
+                out=wo_w[g][:].rearrange("p a n -> p (a n)").bitcast(FP8X4),
+                scales=wo_s[g][:].rearrange("p a n -> p (a n)"),
+                in_=wo_bf[g][:].rearrange("p a x -> p (a x)"),
+            )
+
+        got_s = [keep.tile([P, 2, JH], U8, name=f"got_s{h}", align_bytes=64) for h in range(HALVES)]
+        got_w = [[keep.tile([P, JH], U32, name=f"got_w{h}{l}", tag=f"slot{h}{l}", align_bytes=64) for l in range(2)] for h in range(HALVES)]
+        parted = [
+            [keep.tile([P, PASSES, 2 * JH], U8, name=f"parted{h}{l}", align_bytes=64) for l in range(2)]
+            for h in range(HALVES)
+        ]
+        half_words = 2 * JH // 4
+
+        def offsets(l, h):
+            return lists[l][:, h * (JH // 16) : (h + 1) * (JH // 16)]
+
+        def gather(h):
+            for l in range(2):
+                nc.vector.tensor_copy(got_s[h][:, l, :], tab_s[:].bitcast(U8).indirect(offsets(l, h)))
+            nc.sync.dma_start(
+                shifted[0:SHIFT_ROWS, h * half_words : (h + 1) * half_words],
+                got_s[h][16:P, :, :].rearrange("p l j -> p (l j)").bitcast(I32),
+            )
+            for l in range(2):
+                nc.vector.tensor_copy(got_w[h][l][:], tab_w[:].bitcast(U32).indirect(offsets(l, h)))
+            for l in range(2):
+                nc.vector.tensor_copy(
+                    parted[h][l][:].bitcast(U16),
+                    got_w[h][l][:].bitcast(U16).rearrange("p (j d) -> p d j", d=PASSES),
+                )
+
+        def table_operand(l, h, a):
+            codes = parted[h][l][:, a, :].bitcast(FP4X4)
+            if a == 0:
+                return codes, got_s[h][:, l, :]
+            first = h * half_words + l * (JH // 4)
+            return codes, shifted[:, first : first + JH // 4].bitcast(U8)
+
+        def weight_operand(name, i, a):
+            if name == "o":
+                g, c = divmod(i * P, NH)
+                return wo_w[g][:, a, c : c + P].bitcast(FP8X4), wo_s[g][:, a, c : c + P]
+            first = ("abc".index(name) * PASSES + a) * N + i * P
+            scales = w_s8[:, first : first + P]
+            if name == "a":
+                return wa_w[:, a, i * P : (i + 1) * P].bitcast(FP8X4), scales
+            words = wb_w if name == "b" else wc_w
+            return words[:, a, i * (P // 2) : (i + 1) * (P // 2)].bitcast(FP4X4), scales
+
+        def product(acc, terms, i, h):
+            passes = [(name, l, a) for a in range(PASSES) for name, l in terms]
+            for s, (name, l, a) in enumerate(passes):
+                w_codes, w_scales = weight_operand(name, i, a)
+                t_codes, t_scales = table_operand(l, h, a)
+                nc.tensor.matmul_mx(
+                    out=acc[:], lhsT=w_codes, lhsT_scale=w_scales, rhs=t_codes, rhs_scale=t_scales,
+                    start=(s == 0), stop=(s == len(passes) - 1),
+                )
+
+        units = [(i, h) for i in range(NT) for h in range(HALVES)]
+        gated = {}
+        own = {}
+        result = {}
+
+        def first_stage(k):
+            i, h = units[k]
+            za = psum.tile([P, JH], F32, name="za", bufs=2)
+            ms = psum.tile([P, JH], F32, name="ms", bufs=3)
+            ow = psum.tile([P, JH], F32, name="ow", bufs=3)
+            product(za, [("a", DST), ("b", SRC)], i, h)
+            product(ms, [("c", SRC)], i, h)
+            product(ow, [("o", DST)], i, h)
+            th = work.tile([P, JH], F32, name="th")
+            nc.scalar.activation(th[:], za[:], ACT.Tanh, scale=0.5)
+            twice = work.tile([P, JH], F32, name="twice")
+            nc.vector.scalar_tensor_tensor(twice[:], th[:], 1.0, ms[:], ALU.add, ALU.mult)
+            gated[k] = twice
+            own[k] = ow
+
+        def second_stage(k):
+            i, h = units[k]
+            u = work.tile([P, JH], F32, name="u")
+            nc.vector.scalar_tensor_tensor(u[:], gated[k][:], 0.5, own[k][:], ALU.mult, ALU.add)
+            r = work.tile([P, JH], F32, name="r")
+            nc.scalar.activation(r[:], u[:], ACT.Silu, bias=bias[:, i : i + 1])
+            result[k] = r
+
+        def third_stage(k):
+            i, h = units[k]
+            window = windows[i % 2]
+            nc.vector.tensor_tensor(
+                window[:].indirect(offsets(DST, h)), result[k][:], edge_w[h][:], ALU.mult
+            )
+            if h == HALVES - 1:
+                nc.sync.dma_start(out[i * P : (i + 1) * P, :], window[:])
+
+        cast_wo(0)
+        gather(0)
+        quantize_wo(0)
+        edge_w = []
+        for h in range(HALVES):
+            part = keep.tile([P, JH], F32, name=f"edge_w{h}", tag=f"slot0{h}", align_bytes=64)
+            nc.sync.dma_start(part[:], wgo[:, h * JH : (h + 1) * JH])
+            edge_w.append(part)
+        gather(1)
+        load_wo(1)
+        cast_wo(1)
+        for step in range(len(units) + 2):
+            if step < len(units):
+                first_stage(step)
+            if 0 <= step - 1 < len(units):
+                second_stage(step - 1)
+            if step == 1:
+                quantize_wo(1)
+            if step - 2 >= 0:
+                third_stage(step - 2)

@@ -32,6 +32,7 @@ def tile_list_rgg_ownsilu_kernel(
     with ExitStack() as ctx:
         keep = ctx.enter_context(tc.tile_pool(name="keep", bufs=1))
         work = ctx.enter_context(tc.tile_pool(name="work", bufs=3))
+        stage = ctx.enter_context(tc.tile_pool(name="stage", bufs=1))
         psum = ctx.enter_context(tc.psum_pool(name="psum", bufs=1))
 
         src_list = keep.tile([P, J // 16], U16, name="src_list")
@@ -43,7 +44,7 @@ def tile_list_rgg_ownsilu_kernel(
         tab_s = keep.tile([P, T // 4], I32, name="tab_s", align_bytes=64)
         w_s = keep.tile([P, 3 * PASSES * N // 4], I32, name="w_s", align_bytes=64)
         shifted = keep.tile([P, HALVES * 2 * JH // 4 + 1], I32, name="shifted", align_bytes=64)
-        windows = [keep.tile([P, T], F32, name=f"window{i}", align_bytes=64) for i in range(2)]
+        windows = [keep.tile([P, T], F32, name=f"window{i}", align_bytes=64) for i in range(3)]
         warm = keep.tile([P, 1], F32, name="warm")
         bias = keep.tile([P, NT], F32, name="bias")
 
@@ -91,7 +92,10 @@ def tile_list_rgg_ownsilu_kernel(
         with nc.allow_non_contiguous_dma(reason="one bias value for each partition and row tile"):
             nc.sync.dma_start(bias[:], b.rearrange("(c p) -> p c", p=P))
 
-        wo_bf = [keep.tile([P, PASSES, NH * 4], BF16, name=f"wo_bf{g}", align_bytes=64) for g in range(N // NH)]
+        wo_bf = [
+            stage.tile([P, PASSES, NH * 4], BF16, name="wo_bf0", align_bytes=64, offset=512),
+            keep.tile([P, PASSES, NH * 4], BF16, name="wo_bf1", align_bytes=64),
+        ]
         wo_w = [keep.tile([P, PASSES, NH], U32, name=f"wo_w{g}", align_bytes=64) for g in range(N // NH)]
         wo_s = [keep.tile([P, PASSES, NH], U8, name=f"wo_s{g}", align_bytes=64) for g in range(N // NH)]
 
@@ -110,8 +114,14 @@ def tile_list_rgg_ownsilu_kernel(
                 in_=wo_bf[g][:].rearrange("p a x -> p (a x)"),
             )
 
-        got_s = [keep.tile([P, 2, JH], U8, name=f"got_s{h}", align_bytes=64) for h in range(HALVES)]
-        got_w = [[keep.tile([P, JH], U32, name=f"got_w{h}{l}", tag=f"slot{h}{l}", align_bytes=64) for l in range(2)] for h in range(HALVES)]
+        got_s = [
+            keep.tile([P, 2, JH], U8, name="got_s0", align_bytes=64),
+            stage.tile([P, 2, JH], U8, name="got_s1", align_bytes=64, offset=0),
+        ]
+        got_w = [
+            [keep.tile([P, JH], U32, name=f"got_w0{l}", align_bytes=64) for l in range(2)],
+            [stage.tile([P, JH], U32, name=f"got_w1{l}", align_bytes=64, offset=1024 + 2048 * l) for l in range(2)],
+        ]
         parted = [
             [keep.tile([P, PASSES, 2 * JH], U8, name=f"parted{h}{l}", align_bytes=64) for l in range(2)]
             for h in range(HALVES)
@@ -164,7 +174,7 @@ def tile_list_rgg_ownsilu_kernel(
                     start=(s == 0), stop=(s == len(passes) - 1),
                 )
 
-        units = [(i, h) for i in range(NT) for h in range(HALVES)]
+        units = [(0, 0), (1, 0), (0, 1), (1, 1), (2, 0), (2, 1), (3, 0), (3, 1)]
         gated = {}
         own = {}
         result = {}
@@ -172,8 +182,8 @@ def tile_list_rgg_ownsilu_kernel(
         def first_stage(k):
             i, h = units[k]
             za = psum.tile([P, JH], F32, name="za", bufs=2)
-            ms = psum.tile([P, JH], F32, name="ms", bufs=3)
-            ow = psum.tile([P, JH], F32, name="ow", bufs=3)
+            ms = psum.tile([P, JH], F32, name="ms", bufs=2)
+            ow = psum.tile([P, JH], F32, name="ow", bufs=2)
             product(za, [("a", DST), ("b", SRC)], i, h)
             product(ms, [("c", SRC)], i, h)
             product(ow, [("o", DST)], i, h)
@@ -181,34 +191,33 @@ def tile_list_rgg_ownsilu_kernel(
             nc.scalar.activation(th[:], za[:], ACT.Tanh, scale=0.5)
             twice = work.tile([P, JH], F32, name="twice")
             nc.vector.scalar_tensor_tensor(twice[:], th[:], 1.0, ms[:], ALU.add, ALU.mult)
+            own_twice = work.tile([P, JH], F32, name="own_twice")
+            nc.scalar.activation(own_twice[:], ow[:], ACT.Copy, scale=2.0)
             gated[k] = twice
-            own[k] = ow
+            own[k] = own_twice
 
         def second_stage(k):
             i, h = units[k]
             u = work.tile([P, JH], F32, name="u")
-            nc.vector.scalar_tensor_tensor(u[:], gated[k][:], 0.5, own[k][:], ALU.mult, ALU.add)
+            nc.gpsimd.tensor_tensor(u[:], gated[k][:], own[k][:], ALU.add)
             r = work.tile([P, JH], F32, name="r")
-            nc.scalar.activation(r[:], u[:], ACT.Silu, bias=bias[:, i : i + 1])
-            result[k] = r
+            nc.scalar.activation(r[:], u[:], ACT.Silu, bias=bias[:, i : i + 1], scale=0.5)
+            rw = work.tile([P, JH], F32, name="rw")
+            nc.gpsimd.tensor_tensor(rw[:], r[:], edge_w[:, h * JH : (h + 1) * JH], ALU.mult)
+            result[k] = rw
 
         def third_stage(k):
             i, h = units[k]
-            window = windows[i % 2]
-            nc.vector.tensor_tensor(
-                window[:].indirect(offsets(DST, h)), result[k][:], edge_w[h][:], ALU.mult
-            )
+            window = windows[i % 3]
+            nc.vector.tensor_copy(window[:].indirect(offsets(DST, h)), result[k][:])
             if h == HALVES - 1:
                 nc.sync.dma_start(out[i * P : (i + 1) * P, :], window[:])
 
         cast_wo(0)
         gather(0)
         quantize_wo(0)
-        edge_w = []
-        for h in range(HALVES):
-            part = keep.tile([P, JH], F32, name=f"edge_w{h}", tag=f"slot0{h}", align_bytes=64)
-            nc.sync.dma_start(part[:], wgo[:, h * JH : (h + 1) * JH])
-            edge_w.append(part)
+        edge_w = keep.tile([P, J], F32, name="edge_w", align_bytes=64)
+        nc.sync.dma_start(edge_w[:], wgo)
         gather(1)
         load_wo(1)
         cast_wo(1)

@@ -31,7 +31,8 @@ def tile_list_rgg_ownsilu_kernel(
     nc = tc.nc
     with ExitStack() as ctx:
         keep = ctx.enter_context(tc.tile_pool(name="keep", bufs=1))
-        work = ctx.enter_context(tc.tile_pool(name="work", bufs=3))
+        work = ctx.enter_context(tc.tile_pool(name="work", bufs=4))
+        ring = ctx.enter_context(tc.tile_pool(name="ring", bufs=1))
         stage = ctx.enter_context(tc.tile_pool(name="stage", bufs=1))
         psum = ctx.enter_context(tc.psum_pool(name="psum", bufs=1))
 
@@ -44,16 +45,18 @@ def tile_list_rgg_ownsilu_kernel(
         tab_s = keep.tile([P, T // 4], I32, name="tab_s", align_bytes=64)
         w_s = keep.tile([P, 3 * PASSES * N // 4], I32, name="w_s", align_bytes=64)
         shifted = keep.tile([P, HALVES * 2 * JH // 4 + 1], I32, name="shifted", align_bytes=64)
-        windows = [keep.tile([P, T], F32, name=f"window{i}", align_bytes=64) for i in range(3)]
+        windows = [keep.tile([P, T], F32, name=f"window{i}", align_bytes=64) for i in range(NT)]
         warm = keep.tile([P, 1], F32, name="warm")
         bias = keep.tile([P, NT], F32, name="bias")
 
         nc.gpsimd.memset(tab_s[:], 0)
         nc.gpsimd.memset(w_s[:], 0)
-        for window in windows:
+        for window in windows[:-1]:
             nc.gpsimd.memset(window[:], 0.0)
         nc.vector.memset(warm[:], 0.0)
         nc.vector.memset(shifted[:], 0)
+        nc.vector.memset(windows[-1][:, 0 : T // 2 - 1], 0.0)
+        nc.vector.memset(windows[-1][:, T // 2 - 1 : T], 0.0)
         nc.scalar.activation(warm[:], warm[:], ACT.Silu)
 
         nc.sync.dma_start(dst_list[:], offs2)
@@ -123,28 +126,34 @@ def tile_list_rgg_ownsilu_kernel(
             [stage.tile([P, JH], U32, name=f"got_w1{l}", align_bytes=64, offset=1024 + 2048 * l) for l in range(2)],
         ]
         parted = [
-            [keep.tile([P, PASSES, 2 * JH], U8, name=f"parted{h}{l}", align_bytes=64) for l in range(2)]
-            for h in range(HALVES)
+            [keep.tile([P, PASSES, 2 * JH], U8, name=f"parted0{l}", align_bytes=64) for l in range(2)],
+            [
+                stage.tile([P, PASSES, 2 * JH], U8, name=f"parted1{l}", align_bytes=64, offset=8192 + 2048 * l)
+                for l in range(2)
+            ],
         ]
+        early_gate_offsets = (4608, 8192, 10240)
         half_words = 2 * JH // 4
 
         def offsets(l, h):
             return lists[l][:, h * (JH // 16) : (h + 1) * (JH // 16)]
 
-        def gather(h):
+        def gather_scales(h):
             for l in range(2):
                 nc.vector.tensor_copy(got_s[h][:, l, :], tab_s[:].bitcast(U8).indirect(offsets(l, h)))
             nc.sync.dma_start(
                 shifted[0:SHIFT_ROWS, h * half_words : (h + 1) * half_words],
                 got_s[h][16:P, :, :].rearrange("p l j -> p (l j)").bitcast(I32),
             )
-            for l in range(2):
-                nc.vector.tensor_copy(got_w[h][l][:], tab_w[:].bitcast(U32).indirect(offsets(l, h)))
-            for l in range(2):
-                nc.vector.tensor_copy(
-                    parted[h][l][:].bitcast(U16),
-                    got_w[h][l][:].bitcast(U16).rearrange("p (j d) -> p d j", d=PASSES),
-                )
+
+        def gather_words(h, l):
+            nc.vector.tensor_copy(got_w[h][l][:], tab_w[:].bitcast(U32).indirect(offsets(l, h)))
+
+        def part_words(h, l):
+            nc.vector.tensor_copy(
+                parted[h][l][:].bitcast(U16),
+                got_w[h][l][:].bitcast(U16).rearrange("p (j d) -> p d j", d=PASSES),
+            )
 
         def table_operand(l, h, a):
             codes = parted[h][l][:, a, :].bitcast(FP4X4)
@@ -174,59 +183,82 @@ def tile_list_rgg_ownsilu_kernel(
                     start=(s == 0), stop=(s == len(passes) - 1),
                 )
 
-        units = [(0, 0), (1, 0), (0, 1), (1, 1), (2, 0), (2, 1), (3, 0), (3, 1)]
+        units = [(i, h) for h in range(HALVES) for i in range(NT)]
         gated = {}
         own = {}
         result = {}
 
-        def first_stage(k):
+        def gate(k):
             i, h = units[k]
-            za = psum.tile([P, JH], F32, name="za", bufs=2)
-            ms = psum.tile([P, JH], F32, name="ms", bufs=2)
-            ow = psum.tile([P, JH], F32, name="ow", bufs=2)
+            za = psum.tile([P, JH], F32, name=f"za{k}", offset=2048 * (k % 5))
+            ms = psum.tile([P, JH], F32, name=f"ms{k}", offset=2048 * (5 + k % 3))
             product(za, [("a", DST), ("b", SRC)], i, h)
             product(ms, [("c", SRC)], i, h)
-            product(ow, [("o", DST)], i, h)
-            th = work.tile([P, JH], F32, name="th")
+            if k < len(early_gate_offsets):
+                th = stage.tile([P, JH], F32, name=f"th{k}", align_bytes=64, offset=early_gate_offsets[k])
+            else:
+                th = work.tile([P, JH], F32, name="th")
             nc.scalar.activation(th[:], za[:], ACT.Tanh, scale=0.5)
             twice = work.tile([P, JH], F32, name="twice")
             nc.vector.scalar_tensor_tensor(twice[:], th[:], 1.0, ms[:], ALU.add, ALU.mult)
+            gated[k] = twice
+
+        def project(k):
+            i, h = units[k]
+            ow = psum.tile([P, JH], F32, name=f"ow{k}", offset=2048 * ((k + 1) % 5))
+            product(ow, [("o", DST)], i, h)
             own_twice = work.tile([P, JH], F32, name="own_twice")
             nc.scalar.activation(own_twice[:], ow[:], ACT.Copy, scale=2.0)
-            gated[k] = twice
             own[k] = own_twice
 
-        def second_stage(k):
+        def finish(k):
             i, h = units[k]
-            u = work.tile([P, JH], F32, name="u")
+            u = ring.tile([P, JH], F32, name=f"u{k}", offset=4 * JH * (k % 4))
             nc.gpsimd.tensor_tensor(u[:], gated[k][:], own[k][:], ALU.add)
-            r = work.tile([P, JH], F32, name="r")
+            r = ring.tile([P, JH], F32, name=f"r{k}", offset=4 * JH * ((k + 2) % 4))
             nc.scalar.activation(r[:], u[:], ACT.Silu, bias=bias[:, i : i + 1], scale=0.5)
             rw = work.tile([P, JH], F32, name="rw")
-            nc.gpsimd.tensor_tensor(rw[:], r[:], edge_w[:, h * JH : (h + 1) * JH], ALU.mult)
+            nc.gpsimd.tensor_tensor(rw[:], r[:], edge_w[h][:], ALU.mult)
             result[k] = rw
 
-        def third_stage(k):
+        def scatter(k):
             i, h = units[k]
-            window = windows[i % 3]
-            nc.vector.tensor_copy(window[:].indirect(offsets(DST, h)), result[k][:])
+            nc.vector.tensor_copy(windows[i][:].indirect(offsets(DST, h)), result[k][:])
             if h == HALVES - 1:
-                nc.sync.dma_start(out[i * P : (i + 1) * P, :], window[:])
+                nc.sync.dma_start(out[i * P : (i + 1) * P, :], windows[i][:])
+
+        edge_w = {}
+
+        def load_edge_weights(h, name):
+            edge_w[h] = keep.tile([P, JH], F32, name=name)
+            nc.sync.dma_start(edge_w[h][:], wgo[:, h * JH : (h + 1) * JH])
 
         cast_wo(0)
-        gather(0)
+        gather_scales(0)
+        for l in range(2):
+            gather_words(0, l)
+        for l in range(2):
+            part_words(0, l)
         quantize_wo(0)
-        edge_w = keep.tile([P, J], F32, name="edge_w", align_bytes=64)
-        nc.sync.dma_start(edge_w[:], wgo)
-        gather(1)
+        load_edge_weights(0, "edge_w0")
         load_wo(1)
+        gather_scales(1)
+        gather_words(1, DST)
+        gate(0)
+        gather_words(1, SRC)
+        gate(1)
+        project(0)
+        finish(0)
+        part_words(1, DST)
+        gate(2)
+        part_words(1, SRC)
         cast_wo(1)
-        for step in range(len(units) + 2):
-            if step < len(units):
-                first_stage(step)
-            if 0 <= step - 1 < len(units):
-                second_stage(step - 1)
-            if step == 1:
-                quantize_wo(1)
-            if step - 2 >= 0:
-                third_stage(step - 2)
+        load_edge_weights(1, "wo_raw0")
+        quantize_wo(1)
+        for step in range(2, len(units) + 2):
+            if 2 < step < len(units):
+                gate(step)
+            if step - 1 < len(units):
+                project(step - 1)
+                finish(step - 1)
+            scatter(step - 2)

@@ -45,9 +45,8 @@ def tile_list_rgg_ownsilu_kernel(
         tab_s = keep.tile([P, T // 4], I32, name="tab_s", align_bytes=64)
         w_s = keep.tile([P, 3 * PASSES * N // 4], I32, name="w_s", align_bytes=64)
         shifted = keep.tile([P, HALVES * 2 * JH // 4 + 1], I32, name="shifted", align_bytes=64)
-        windows = [keep.tile([P, T], F32, name=f"window{i}", align_bytes=64) for i in range(NT)]
+        windows = [keep.tile([P, T], F32, name=f"window{i}", align_bytes=64) for i in range(3)]
         warm = keep.tile([P, 1], F32, name="warm")
-        bias = keep.tile([P, NT], F32, name="bias")
 
         nc.gpsimd.memset(tab_s[:], 0)
         nc.gpsimd.memset(w_s[:], 0)
@@ -78,7 +77,7 @@ def tile_list_rgg_ownsilu_kernel(
         wo_raw = {}
 
         def load_wo(g):
-            wo_raw[g] = [keep.tile([P, 4, NH], F32, name=f"wo_raw{a}") for a in range(PASSES)]
+            wo_raw[g] = [keep.tile([P, 4, NH], F32, name=f"wo_raw{a}", tag=f"wo_raw{a}") for a in range(PASSES)]
             for a in range(PASSES):
                 rows = wo[512 * a : 512 * (a + 1), g * NH : (g + 1) * NH]
                 nc.sync.dma_start(wo_raw[g][a][:], rows.rearrange("(p i) n -> p i n", i=4))
@@ -92,12 +91,10 @@ def tile_list_rgg_ownsilu_kernel(
         nc.sync.dma_start(wa_w[:], wa_words.rearrange("a p n i -> p a (n i)").bitcast(I32))
         nc.sync.dma_start(wb_w[:], wb_words.rearrange("a p x -> p a x").bitcast(I32))
         nc.sync.dma_start(wc_w[:], wc_words.rearrange("a p x -> p a x").bitcast(I32))
-        with nc.allow_non_contiguous_dma(reason="one bias value for each partition and row tile"):
-            nc.sync.dma_start(bias[:], b.rearrange("(c p) -> p c", p=P))
 
         wo_bf = [
             stage.tile([P, PASSES, NH * 4], BF16, name="wo_bf0", align_bytes=64, offset=512),
-            keep.tile([P, PASSES, NH * 4], BF16, name="wo_bf1", align_bytes=64),
+            stage.tile([P, PASSES, NH * 4], BF16, name="wo_bf1", align_bytes=64, offset=8192),
         ]
         wo_w = [keep.tile([P, PASSES, NH], U32, name=f"wo_w{g}", align_bytes=64) for g in range(N // NH)]
         wo_s = [keep.tile([P, PASSES, NH], U8, name=f"wo_s{g}", align_bytes=64) for g in range(N // NH)]
@@ -126,13 +123,9 @@ def tile_list_rgg_ownsilu_kernel(
             [stage.tile([P, JH], U32, name=f"got_w1{l}", align_bytes=64, offset=1024 + 2048 * l) for l in range(2)],
         ]
         parted = [
-            [keep.tile([P, PASSES, 2 * JH], U8, name=f"parted0{l}", align_bytes=64) for l in range(2)],
-            [
-                stage.tile([P, PASSES, 2 * JH], U8, name=f"parted1{l}", align_bytes=64, offset=8192 + 2048 * l)
-                for l in range(2)
-            ],
+            [keep.tile([P, PASSES, 2 * JH], U8, name=f"parted{h}{l}", align_bytes=64) for l in range(2)]
+            for h in range(HALVES)
         ]
-        early_gate_offsets = (4608, 8192, 10240)
         half_words = 2 * JH // 4
 
         def offsets(l, h):
@@ -183,21 +176,20 @@ def tile_list_rgg_ownsilu_kernel(
                     start=(s == 0), stop=(s == len(passes) - 1),
                 )
 
-        units = [(i, h) for h in range(HALVES) for i in range(NT)]
+        units = [(2 * g + i, h) for g in range(2) for h in range(HALVES) for i in range(2)]
+        gate_bank = (0, 1, 0, 1, 2, 3, 0, 1)
+        own_bank = (2, 3) + gate_bank[3:] + (2,)
         gated = {}
         own = {}
         result = {}
 
         def gate(k):
             i, h = units[k]
-            za = psum.tile([P, JH], F32, name=f"za{k}", offset=2048 * (k % 5))
-            ms = psum.tile([P, JH], F32, name=f"ms{k}", offset=2048 * (5 + k % 3))
+            za = psum.tile([P, JH], F32, name=f"za{k}", offset=2048 * gate_bank[k])
+            ms = psum.tile([P, JH], F32, name=f"ms{k}", offset=2048 * (4 + k % 2))
             product(za, [("a", DST), ("b", SRC)], i, h)
             product(ms, [("c", SRC)], i, h)
-            if k < len(early_gate_offsets):
-                th = stage.tile([P, JH], F32, name=f"th{k}", align_bytes=64, offset=early_gate_offsets[k])
-            else:
-                th = work.tile([P, JH], F32, name="th")
+            th = work.tile([P, JH], F32, name="th")
             nc.scalar.activation(th[:], za[:], ACT.Tanh, scale=0.5)
             twice = work.tile([P, JH], F32, name="twice")
             nc.vector.scalar_tensor_tensor(twice[:], th[:], 1.0, ms[:], ALU.add, ALU.mult)
@@ -205,60 +197,75 @@ def tile_list_rgg_ownsilu_kernel(
 
         def project(k):
             i, h = units[k]
-            ow = psum.tile([P, JH], F32, name=f"ow{k}", offset=2048 * ((k + 1) % 5))
+            ow = psum.tile([P, JH], F32, name=f"ow{k}", offset=2048 * own_bank[k])
             product(ow, [("o", DST)], i, h)
+            if k == 0:
+                own[k] = ow
+                return
             own_twice = work.tile([P, JH], F32, name="own_twice")
             nc.scalar.activation(own_twice[:], ow[:], ACT.Copy, scale=2.0)
             own[k] = own_twice
 
-        def finish(k):
+        def activate(k):
             i, h = units[k]
             u = ring.tile([P, JH], F32, name=f"u{k}", offset=4 * JH * (k % 4))
-            nc.gpsimd.tensor_tensor(u[:], gated[k][:], own[k][:], ALU.add)
-            r = ring.tile([P, JH], F32, name=f"r{k}", offset=4 * JH * ((k + 2) % 4))
+            if k == 0:
+                nc.vector.scalar_tensor_tensor(u[:], own[k][:], 2.0, gated[k][:], ALU.mult, ALU.add)
+            else:
+                nc.gpsimd.tensor_tensor(u[:], gated[k][:], own[k][:], ALU.add)
+            r = ring.tile([P, JH], F32, name=f"r{k}", offset=4 * JH * (1 if k == 0 else (k + 2) % 4))
             nc.scalar.activation(r[:], u[:], ACT.Silu, bias=bias[:, i : i + 1], scale=0.5)
-            rw = work.tile([P, JH], F32, name="rw")
-            nc.gpsimd.tensor_tensor(rw[:], r[:], edge_w[h][:], ALU.mult)
+            result[k] = r
+
+        def weigh(k):
+            i, h = units[k]
+            if k == 0:
+                rw = stage.tile([P, JH], F32, name="rw0", align_bytes=64, offset=8192)
+                nc.vector.tensor_tensor(rw[:], result[k][:], edge_w[h][:], ALU.mult)
+            else:
+                rw = work.tile([P, JH], F32, name="rw")
+                nc.gpsimd.tensor_tensor(rw[:], result[k][:], edge_w[h][:], ALU.mult)
             result[k] = rw
 
         def scatter(k):
             i, h = units[k]
-            nc.vector.tensor_copy(windows[i][:].indirect(offsets(DST, h)), result[k][:])
+            nc.vector.tensor_copy(windows[i % 3][:].indirect(offsets(DST, h)), result[k][:])
             if h == HALVES - 1:
-                nc.sync.dma_start(out[i * P : (i + 1) * P, :], windows[i][:])
+                nc.sync.dma_start(out[i * P : (i + 1) * P, :], windows[i % 3][:])
 
-        edge_w = {}
-
-        def load_edge_weights(h, name):
-            edge_w[h] = keep.tile([P, JH], F32, name=name)
-            nc.sync.dma_start(edge_w[h][:], wgo[:, h * JH : (h + 1) * JH])
-
+        edge_w = [keep.tile([P, JH], F32, name=f"edge_w{h}") for h in range(HALVES)]
+        bias = keep.tile([P, NT], F32, name="bias")
         cast_wo(0)
         gather_scales(0)
+        nc.sync.dma_start(edge_w[0][:], wgo[:, 0:JH])
+        load_wo(1)
+        with nc.allow_non_contiguous_dma(reason="one bias value for each partition and row tile"):
+            nc.sync.dma_start(bias[:], b.rearrange("(c p) -> p c", p=P))
         for l in range(2):
             gather_words(0, l)
         for l in range(2):
             part_words(0, l)
         quantize_wo(0)
-        load_edge_weights(0, "edge_w0")
-        load_wo(1)
         gather_scales(1)
-        gather_words(1, DST)
+        nc.sync.dma_start(edge_w[1][:], wgo[:, JH:J])
+        for l in range(2):
+            gather_words(1, l)
+        for l in range(2):
+            part_words(1, l)
         gate(0)
-        gather_words(1, SRC)
-        gate(1)
         project(0)
-        finish(0)
-        part_words(1, DST)
-        gate(2)
-        part_words(1, SRC)
+        activate(0)
         cast_wo(1)
-        load_edge_weights(1, "wo_raw0")
         quantize_wo(1)
+        gate(1)
+        project(1)
+        weigh(0)
         for step in range(2, len(units) + 2):
-            if 2 < step < len(units):
+            if step < len(units):
                 gate(step)
-            if step - 1 < len(units):
+            if 2 <= step - 1 < len(units):
                 project(step - 1)
-                finish(step - 1)
+            if step - 1 < len(units):
+                activate(step - 1)
+                weigh(step - 1)
             scatter(step - 2)

@@ -32,7 +32,6 @@ def tile_list_rgg_ownsilu_kernel(
     with ExitStack() as ctx:
         keep = ctx.enter_context(tc.tile_pool(name="keep", bufs=1))
         work = ctx.enter_context(tc.tile_pool(name="work", bufs=4))
-        ring = ctx.enter_context(tc.tile_pool(name="ring", bufs=1))
         stage = ctx.enter_context(tc.tile_pool(name="stage", bufs=1))
         psum = ctx.enter_context(tc.psum_pool(name="psum", bufs=1))
 
@@ -45,7 +44,7 @@ def tile_list_rgg_ownsilu_kernel(
         tab_s = keep.tile([P, T // 4], I32, name="tab_s", align_bytes=64)
         w_s = keep.tile([P, 3 * PASSES * N // 4], I32, name="w_s", align_bytes=64)
         shifted = keep.tile([P, HALVES * 2 * JH // 4 + 1], I32, name="shifted", align_bytes=64)
-        windows = [keep.tile([P, T], F32, name=f"window{i}", align_bytes=64) for i in range(3)]
+        windows = [keep.tile([P, T], F32, name=f"window{i}", align_bytes=64) for i in range(NT)]
         warm = keep.tile([P, 1], F32, name="warm")
 
         nc.gpsimd.memset(tab_s[:], 0)
@@ -74,10 +73,9 @@ def tile_list_rgg_ownsilu_kernel(
             )
         w_s8 = w_s[:].bitcast(U8)
 
-        wo_raw = {}
+        wo_raw = [[keep.tile([P, 4, NH], F32, name=f"wo_raw{g}{a}") for a in range(PASSES)] for g in range(N // NH)]
 
         def load_wo(g):
-            wo_raw[g] = [keep.tile([P, 4, NH], F32, name=f"wo_raw{a}", tag=f"wo_raw{a}") for a in range(PASSES)]
             for a in range(PASSES):
                 rows = wo[512 * a : 512 * (a + 1), g * NH : (g + 1) * NH]
                 nc.sync.dma_start(wo_raw[g][a][:], rows.rearrange("(p i) n -> p i n", i=4))
@@ -85,16 +83,23 @@ def tile_list_rgg_ownsilu_kernel(
         wa_w = keep.tile([P, PASSES, N], I32, name="wa_w", align_bytes=64)
         wb_w = keep.tile([P, PASSES, N // 2], I32, name="wb_w", align_bytes=64)
         wc_w = keep.tile([P, PASSES, N // 2], I32, name="wc_w", align_bytes=64)
+        edge_w = [keep.tile([P, JH], F32, name=f"edge_w{h}") for h in range(HALVES)]
+        bias = keep.tile([P, NT], F32, name="bias")
         load_wo(0)
         for q in range(4):
-            nc.sync.dma_start(w_s[32 * q : 32 * q + 4, :], w_rows[4 * q : 4 * q + 4, :])
+            nc.scalar.dma_start(w_s[32 * q : 32 * q + 4, :], w_rows[4 * q : 4 * q + 4, :])
         nc.sync.dma_start(wa_w[:], wa_words.rearrange("a p n i -> p a (n i)").bitcast(I32))
         nc.sync.dma_start(wb_w[:], wb_words.rearrange("a p x -> p a x").bitcast(I32))
         nc.sync.dma_start(wc_w[:], wc_words.rearrange("a p x -> p a x").bitcast(I32))
+        load_wo(1)
+        with nc.allow_non_contiguous_dma(reason="one bias value for each partition and row tile"):
+            nc.sync.dma_start(bias[:], b.rearrange("(c p) -> p c", p=P))
+        for h in range(HALVES):
+            nc.sync.dma_start(edge_w[h][:], wgo[:, h * JH : (h + 1) * JH])
 
         wo_bf = [
-            stage.tile([P, PASSES, NH * 4], BF16, name="wo_bf0", align_bytes=64, offset=512),
-            stage.tile([P, PASSES, NH * 4], BF16, name="wo_bf1", align_bytes=64, offset=8192),
+            stage.tile([P, PASSES, NH * 4], BF16, name=f"wo_bf{g}", align_bytes=64, offset=4096 * g)
+            for g in range(N // NH)
         ]
         wo_w = [keep.tile([P, PASSES, NH], U32, name=f"wo_w{g}", align_bytes=64) for g in range(N // NH)]
         wo_s = [keep.tile([P, PASSES, NH], U8, name=f"wo_s{g}", align_bytes=64) for g in range(N // NH)]
@@ -116,16 +121,13 @@ def tile_list_rgg_ownsilu_kernel(
 
         got_s = [
             keep.tile([P, 2, JH], U8, name="got_s0", align_bytes=64),
-            stage.tile([P, 2, JH], U8, name="got_s1", align_bytes=64, offset=0),
+            stage.tile([P, 2, JH], U8, name="got_s1", align_bytes=64, offset=8192),
         ]
         got_w = [
-            [keep.tile([P, JH], U32, name=f"got_w0{l}", align_bytes=64) for l in range(2)],
-            [stage.tile([P, JH], U32, name=f"got_w1{l}", align_bytes=64, offset=1024 + 2048 * l) for l in range(2)],
+            keep.tile([P, 2, JH], U32, name="got_w0", align_bytes=64),
+            stage.tile([P, 2, JH], U32, name="got_w1", align_bytes=64, offset=0),
         ]
-        parted = [
-            [keep.tile([P, PASSES, 2 * JH], U8, name=f"parted{h}{l}", align_bytes=64) for l in range(2)]
-            for h in range(HALVES)
-        ]
+        parted = [keep.tile([P, 2, PASSES, 2 * JH], U8, name=f"parted{h}", align_bytes=64) for h in range(HALVES)]
         half_words = 2 * JH // 4
 
         def offsets(l, h):
@@ -134,22 +136,22 @@ def tile_list_rgg_ownsilu_kernel(
         def gather_scales(h):
             for l in range(2):
                 nc.vector.tensor_copy(got_s[h][:, l, :], tab_s[:].bitcast(U8).indirect(offsets(l, h)))
-            nc.sync.dma_start(
+            queue = nc.scalar if h == 0 else nc.sync
+            queue.dma_start(
                 shifted[0:SHIFT_ROWS, h * half_words : (h + 1) * half_words],
                 got_s[h][16:P, :, :].rearrange("p l j -> p (l j)").bitcast(I32),
             )
 
-        def gather_words(h, l):
-            nc.vector.tensor_copy(got_w[h][l][:], tab_w[:].bitcast(U32).indirect(offsets(l, h)))
-
-        def part_words(h, l):
+        def gather_words(h):
+            for l in range(2):
+                nc.vector.tensor_copy(got_w[h][:, l, :], tab_w[:].bitcast(U32).indirect(offsets(l, h)))
             nc.vector.tensor_copy(
-                parted[h][l][:].bitcast(U16),
-                got_w[h][l][:].bitcast(U16).rearrange("p (j d) -> p d j", d=PASSES),
+                parted[h][:].bitcast(U16),
+                got_w[h][:].bitcast(U16).rearrange("p l (j d) -> p l d j", d=PASSES),
             )
 
         def table_operand(l, h, a):
-            codes = parted[h][l][:, a, :].bitcast(FP4X4)
+            codes = parted[h][:, l, a, :].bitcast(FP4X4)
             if a == 0:
                 return codes, got_s[h][:, l, :]
             first = h * half_words + l * (JH // 4)
@@ -176,96 +178,100 @@ def tile_list_rgg_ownsilu_kernel(
                     start=(s == 0), stop=(s == len(passes) - 1),
                 )
 
-        units = [(2 * g + i, h) for g in range(2) for h in range(HALVES) for i in range(2)]
-        gate_bank = (0, 1, 0, 1, 2, 3, 0, 1)
-        own_bank = (2, 3) + gate_bank[3:] + (2,)
+        units = [(i, h) for h in range(HALVES) for i in range(NT)]
+        last = len(units) - 1
+        ON_VECTOR = 3
+        sums = {}
         gated = {}
         own = {}
         result = {}
 
-        def gate(k):
+        def multiply(k):
             i, h = units[k]
-            za = psum.tile([P, JH], F32, name=f"za{k}", offset=2048 * gate_bank[k])
-            ms = psum.tile([P, JH], F32, name=f"ms{k}", offset=2048 * (4 + k % 2))
+            za = psum.tile([P, JH], F32, name=f"za{k}", offset=2048 * (k % 2))
+            ms = psum.tile([P, JH], F32, name=f"ms{k}", offset=2048 * (2 + k % 3))
+            ow = psum.tile([P, JH], F32, name=f"ow{k}", offset=2048 * (5 + k % 3))
             product(za, [("a", DST), ("b", SRC)], i, h)
             product(ms, [("c", SRC)], i, h)
-            th = work.tile([P, JH], F32, name="th")
-            nc.scalar.activation(th[:], za[:], ACT.Tanh, scale=0.5)
-            twice = work.tile([P, JH], F32, name="twice")
-            nc.vector.scalar_tensor_tensor(twice[:], th[:], 1.0, ms[:], ALU.add, ALU.mult)
-            gated[k] = twice
-
-        def project(k):
-            i, h = units[k]
-            ow = psum.tile([P, JH], F32, name=f"ow{k}", offset=2048 * own_bank[k])
             product(ow, [("o", DST)], i, h)
             if k == 0:
+                th = stage.tile([P, JH], F32, name="th0", align_bytes=64, offset=8192)
+            else:
+                th = work.tile([P, JH], F32, name="th")
+            nc.scalar.activation(th[:], za[:], ACT.Tanh, scale=0.5)
+            if k < ON_VECTOR:
+                sums[k] = (th, ms)
+            else:
+                eta = work.tile([P, JH], F32, name="eta")
+                nc.scalar.activation(eta[:], th[:], ACT.Copy, scale=0.5, bias=0.5)
+                ms_sb = work.tile([P, JH], F32, name="ms_sb")
+                nc.scalar.activation(ms_sb[:], ms[:], ACT.Copy)
+                sums[k] = (eta, ms_sb)
+            if k == 0:
                 own[k] = ow
-                return
-            own_twice = work.tile([P, JH], F32, name="own_twice")
-            nc.scalar.activation(own_twice[:], ow[:], ACT.Copy, scale=2.0)
-            own[k] = own_twice
+            else:
+                own[k] = work.tile([P, JH], F32, name="own_sb")
+                nc.scalar.activation(own[k][:], ow[:], ACT.Copy, scale=2.0 if k < ON_VECTOR else 1.0)
+
+        def gate(k):
+            if k == 0:
+                gated[k] = stage.tile([P, JH], F32, name="gated0", align_bytes=64, offset=4096)
+            else:
+                gated[k] = work.tile([P, JH], F32, name="gated")
+            if k < ON_VECTOR:
+                nc.vector.scalar_tensor_tensor(gated[k][:], sums[k][0][:], 1.0, sums[k][1][:], ALU.add, ALU.mult)
+            else:
+                nc.gpsimd.tensor_tensor(gated[k][:], sums[k][0][:], sums[k][1][:], ALU.mult)
 
         def activate(k):
             i, h = units[k]
-            u = ring.tile([P, JH], F32, name=f"u{k}", offset=4 * JH * (k % 4))
+            u = work.tile([P, JH], F32, name="u")
             if k == 0:
                 nc.vector.scalar_tensor_tensor(u[:], own[k][:], 2.0, gated[k][:], ALU.mult, ALU.add)
             else:
                 nc.gpsimd.tensor_tensor(u[:], gated[k][:], own[k][:], ALU.add)
-            r = ring.tile([P, JH], F32, name=f"r{k}", offset=4 * JH * (1 if k == 0 else (k + 2) % 4))
-            nc.scalar.activation(r[:], u[:], ACT.Silu, bias=bias[:, i : i + 1], scale=0.5)
-            result[k] = r
+            result[k] = work.tile([P, JH], F32, name="r")
+            nc.scalar.activation(
+                result[k][:], u[:], ACT.Silu, bias=bias[:, i : i + 1], scale=0.5 if k < ON_VECTOR else 1.0
+            )
 
         def weigh(k):
             i, h = units[k]
-            if k == 0:
-                rw = stage.tile([P, JH], F32, name="rw0", align_bytes=64, offset=8192)
-                nc.vector.tensor_tensor(rw[:], result[k][:], edge_w[h][:], ALU.mult)
-            else:
+            if k < last:
                 rw = work.tile([P, JH], F32, name="rw")
                 nc.gpsimd.tensor_tensor(rw[:], result[k][:], edge_w[h][:], ALU.mult)
-            result[k] = rw
+                result[k] = rw
 
         def scatter(k):
             i, h = units[k]
-            nc.vector.tensor_copy(windows[i % 3][:].indirect(offsets(DST, h)), result[k][:])
+            places = windows[i][:].indirect(offsets(DST, h))
+            if k < last:
+                nc.vector.tensor_copy(places, result[k][:])
+            else:
+                nc.vector.tensor_tensor(places, result[k][:], edge_w[h][:], ALU.mult)
             if h == HALVES - 1:
-                nc.sync.dma_start(out[i * P : (i + 1) * P, :], windows[i % 3][:])
+                nc.sync.dma_start(out[i * P : (i + 1) * P, :], windows[i][:])
 
-        edge_w = [keep.tile([P, JH], F32, name=f"edge_w{h}") for h in range(HALVES)]
-        bias = keep.tile([P, NT], F32, name="bias")
         cast_wo(0)
         gather_scales(0)
-        nc.sync.dma_start(edge_w[0][:], wgo[:, 0:JH])
-        load_wo(1)
-        with nc.allow_non_contiguous_dma(reason="one bias value for each partition and row tile"):
-            nc.sync.dma_start(bias[:], b.rearrange("(c p) -> p c", p=P))
-        for l in range(2):
-            gather_words(0, l)
-        for l in range(2):
-            part_words(0, l)
+        gather_words(0)
         quantize_wo(0)
-        gather_scales(1)
-        nc.sync.dma_start(edge_w[1][:], wgo[:, JH:J])
-        for l in range(2):
-            gather_words(1, l)
-        for l in range(2):
-            part_words(1, l)
-        gate(0)
-        project(0)
-        activate(0)
+        gather_words(1)
         cast_wo(1)
         quantize_wo(1)
+        multiply(0)
+        gate(0)
+        activate(0)
+        multiply(1)
         gate(1)
-        project(1)
         weigh(0)
-        for step in range(2, len(units) + 2):
-            if step < len(units):
-                gate(step)
-            if 2 <= step - 1 < len(units):
-                project(step - 1)
-            if step - 1 < len(units):
-                activate(step - 1)
-                weigh(step - 1)
-            scatter(step - 2)
+        activate(1)
+        gather_scales(1)
+        for k in range(2, len(units)):
+            multiply(k)
+            gate(k)
+            weigh(k - 1)
+            activate(k)
+            scatter(k - 2)
+        scatter(last - 1)
+        scatter(last)

@@ -1,6 +1,7 @@
 from contextlib import ExitStack
 
 import concourse.mybir as mybir
+from concourse.masks import make_identity
 
 K, N, T, J = 1024, 512, 2048, 1024
 FLOPS = 4 * 2 * K * N * J
@@ -49,6 +50,8 @@ def tile_list_rgg_ownsilu_kernel(
 
         nc.gpsimd.memset(tab_s[:], 0)
         nc.gpsimd.memset(w_s[:], 0)
+        identity = keep.tile([P, P], F32, name="identity")
+        make_identity(nc, identity[:])
         for window in windows[:-1]:
             nc.gpsimd.memset(window[:], 0.0)
         nc.vector.memset(warm[:], 0.0)
@@ -73,60 +76,51 @@ def tile_list_rgg_ownsilu_kernel(
             )
         w_s8 = w_s[:].bitcast(U8)
 
-        wo_raw = [[keep.tile([P, 4, NH], F32, name=f"wo_raw{g}{a}") for a in range(PASSES)] for g in range(N // NH)]
+        wo_first = keep.tile([P, 4, N], F32, name="wo_first")
+        wo_late = [
+            stage.tile([P, 4, NH], F32, name=f"wo_late{g}", offset=12288 - 4096 * g) for g in range(N // NH)
+        ]
 
-        def load_wo(g):
-            for a in range(PASSES):
-                rows = wo[512 * a : 512 * (a + 1), g * NH : (g + 1) * NH]
-                nc.sync.dma_start(wo_raw[g][a][:], rows.rearrange("(p i) n -> p i n", i=4))
+        def wo_rows(a, first, width):
+            return wo[512 * a : 512 * (a + 1), first : first + width].rearrange("(p i) n -> p i n", i=4)
 
         wa_w = keep.tile([P, PASSES, N], I32, name="wa_w", align_bytes=64)
         wb_w = keep.tile([P, PASSES, N // 2], I32, name="wb_w", align_bytes=64)
         wc_w = keep.tile([P, PASSES, N // 2], I32, name="wc_w", align_bytes=64)
-        edge_w = [keep.tile([P, JH], F32, name=f"edge_w{h}") for h in range(HALVES)]
+        edge_all = keep.tile([P, J], F32, name="edge_all")
         bias = keep.tile([P, NT], F32, name="bias")
-        load_wo(0)
-        for q in range(4):
-            nc.scalar.dma_start(w_s[32 * q : 32 * q + 4, :], w_rows[4 * q : 4 * q + 4, :])
+        nc.sync.dma_start(wo_first[:], wo_rows(0, 0, N))
         nc.sync.dma_start(wa_w[:], wa_words.rearrange("a p n i -> p a (n i)").bitcast(I32))
         nc.sync.dma_start(wb_w[:], wb_words.rearrange("a p x -> p a x").bitcast(I32))
-        nc.sync.dma_start(wc_w[:], wc_words.rearrange("a p x -> p a x").bitcast(I32))
-        load_wo(1)
-        with nc.allow_non_contiguous_dma(reason="one bias value for each partition and row tile"):
-            nc.sync.dma_start(bias[:], b.rearrange("(c p) -> p c", p=P))
-        for h in range(HALVES):
-            nc.sync.dma_start(edge_w[h][:], wgo[:, h * JH : (h + 1) * JH])
+        nc.sync.dma_start(wo_late[0][:], wo_rows(1, 0, NH))
+        for q in range(4):
+            nc.sync.dma_start(w_s[32 * q : 32 * q + 4, :], w_rows[4 * q : 4 * q + 4, :])
 
-        wo_bf = [
-            stage.tile([P, PASSES, NH * 4], BF16, name=f"wo_bf{g}", align_bytes=64, offset=4096 * g)
-            for g in range(N // NH)
-        ]
-        wo_w = [keep.tile([P, PASSES, NH], U32, name=f"wo_w{g}", align_bytes=64) for g in range(N // NH)]
-        wo_s = [keep.tile([P, PASSES, NH], U8, name=f"wo_s{g}", align_bytes=64) for g in range(N // NH)]
+        wo_bf = stage.tile([P, PASSES, N * 4], BF16, name="wo_bf", align_bytes=64, offset=0)
+        wo_w = keep.tile([P, PASSES, N], U32, name="wo_w", align_bytes=64)
+        wo_s = keep.tile([P, PASSES, N], U8, name="wo_s", align_bytes=64)
 
-        def cast_wo(g):
+        def cast_wo():
             for a in range(PASSES):
-                nc.scalar.activation(
-                    wo_bf[g][:, a, :].rearrange("p (c e i) -> p c i e", e=4, i=4),
-                    wo_raw[g][a][:].rearrange("p i (c e) -> p c i e", e=4),
-                    ACT.Copy,
-                )
+                for g in range(N // NH):
+                    nc.scalar.activation(
+                        wo_bf[:, a, 4 * NH * g : 4 * NH * (g + 1)].rearrange("p (c e i) -> p c i e", e=4, i=4),
+                        (wo_late[g][:] if a else wo_first[:, :, g * NH : (g + 1) * NH]).rearrange("p i (c e) -> p c i e", e=4),
+                        ACT.Copy,
+                    )
 
-        def quantize_wo(g):
+        def quantize_wo():
             nc.vector.quantize_mx(
-                out=wo_w[g][:].rearrange("p a n -> p (a n)").bitcast(FP8X4),
-                scales=wo_s[g][:].rearrange("p a n -> p (a n)"),
-                in_=wo_bf[g][:].rearrange("p a x -> p (a x)"),
+                out=wo_w[:].rearrange("p a n -> p (a n)").bitcast(FP8X4),
+                scales=wo_s[:].rearrange("p a n -> p (a n)"),
+                in_=wo_bf[:].rearrange("p a x -> p (a x)"),
             )
 
         got_s = [
             keep.tile([P, 2, JH], U8, name="got_s0", align_bytes=64),
-            stage.tile([P, 2, JH], U8, name="got_s1", align_bytes=64, offset=8192),
+            stage.tile([P, 2, JH], U8, name="got_s1", align_bytes=64, offset=16384),
         ]
-        got_w = [
-            keep.tile([P, 2, JH], U32, name="got_w0", align_bytes=64),
-            stage.tile([P, 2, JH], U32, name="got_w1", align_bytes=64, offset=0),
-        ]
+        got_w = [keep.tile([P, 2, JH], U32, name=f"got_w{h}", tag="got_w", align_bytes=64) for h in range(HALVES)]
         parted = [keep.tile([P, 2, PASSES, 2 * JH], U8, name=f"parted{h}", align_bytes=64) for h in range(HALVES)]
         half_words = 2 * JH // 4
 
@@ -136,8 +130,7 @@ def tile_list_rgg_ownsilu_kernel(
         def gather_scales(h):
             for l in range(2):
                 nc.vector.tensor_copy(got_s[h][:, l, :], tab_s[:].bitcast(U8).indirect(offsets(l, h)))
-            queue = nc.scalar if h == 0 else nc.sync
-            queue.dma_start(
+            nc.sync.dma_start(
                 shifted[0:SHIFT_ROWS, h * half_words : (h + 1) * half_words],
                 got_s[h][16:P, :, :].rearrange("p l j -> p (l j)").bitcast(I32),
             )
@@ -150,128 +143,131 @@ def tile_list_rgg_ownsilu_kernel(
                 got_w[h][:].bitcast(U16).rearrange("p l (j d) -> p l d j", d=PASSES),
             )
 
-        def table_operand(l, h, a):
-            codes = parted[h][:, l, a, :].bitcast(FP4X4)
+        def table_operand(l, block, a):
+            h, first = divmod(block * P, JH)
+            codes = parted[h][:, l, a, 2 * first : 2 * (first + P)].bitcast(FP4X4)
             if a == 0:
-                return codes, got_s[h][:, l, :]
-            first = h * half_words + l * (JH // 4)
-            return codes, shifted[:, first : first + JH // 4].bitcast(U8)
+                return codes, got_s[h][:, l, first : first + P]
+            word = h * half_words + (l * JH + first) // 4
+            return codes, shifted[:, word : word + P // 4].bitcast(U8)
 
-        def weight_operand(name, i, a):
+        def weight_operand(name, a):
             if name == "o":
-                g, c = divmod(i * P, NH)
-                return wo_w[g][:, a, c : c + P].bitcast(FP8X4), wo_s[g][:, a, c : c + P]
-            first = ("abc".index(name) * PASSES + a) * N + i * P
-            scales = w_s8[:, first : first + P]
+                return wo_w[:, a, :].bitcast(FP8X4), wo_s[:, a, :]
+            first = ("abc".index(name) * PASSES + a) * N
+            scales = w_s8[:, first : first + N]
             if name == "a":
-                return wa_w[:, a, i * P : (i + 1) * P].bitcast(FP8X4), scales
+                return wa_w[:, a, :].bitcast(FP8X4), scales
             words = wb_w if name == "b" else wc_w
-            return words[:, a, i * (P // 2) : (i + 1) * (P // 2)].bitcast(FP4X4), scales
+            return words[:, a, :].bitcast(FP4X4), scales
 
-        def product(acc, terms, i, h):
+        def product(acc, terms, block):
             passes = [(name, l, a) for a in range(PASSES) for name, l in terms]
             for s, (name, l, a) in enumerate(passes):
-                w_codes, w_scales = weight_operand(name, i, a)
-                t_codes, t_scales = table_operand(l, h, a)
+                w_codes, w_scales = weight_operand(name, a)
+                t_codes, t_scales = table_operand(l, block, a)
                 nc.tensor.matmul_mx(
-                    out=acc[:], lhsT=w_codes, lhsT_scale=w_scales, rhs=t_codes, rhs_scale=t_scales,
+                    out=acc[:], lhsT=t_codes, lhsT_scale=t_scales, rhs=w_codes, rhs_scale=w_scales,
                     start=(s == 0), stop=(s == len(passes) - 1),
                 )
 
-        units = [(i, h) for h in range(HALVES) for i in range(NT)]
-        last = len(units) - 1
-        ON_VECTOR = 3
-        sums = {}
+        BLOCKS = J // P
+        QUARTERS = BLOCKS // 2
+        JQ = 2 * P
+        tanhs = {}
         gated = {}
         own = {}
-        result = {}
+        result = [[keep.tile([P, JH], F32, name=f"result{i}{h}") for h in range(HALVES)] for i in range(NT)]
 
-        def multiply(k):
-            i, h = units[k]
-            za = psum.tile([P, JH], F32, name=f"za{k}", offset=2048 * (k % 2))
-            ms = psum.tile([P, JH], F32, name=f"ms{k}", offset=2048 * (2 + k % 3))
-            ow = psum.tile([P, JH], F32, name=f"ow{k}", offset=2048 * (5 + k % 3))
-            product(za, [("a", DST), ("b", SRC)], i, h)
-            product(ms, [("c", SRC)], i, h)
-            product(ow, [("o", DST)], i, h)
-            if k == 0:
-                th = stage.tile([P, JH], F32, name="th0", align_bytes=64, offset=8192)
+        def gate_sums(k):
+            za = psum.tile([P, N], F32, name=f"za{k}", offset=2048 * (k % 2))
+            ms = psum.tile([P, N], F32, name=f"ms{k}", offset=2048 * (2 + k % 2))
+            product(za, [("a", DST), ("b", SRC)], k)
+            product(ms, [("c", SRC)], k)
+            if k < 2:
+                th = stage.tile([P, N], F32, name=f"th{k}", align_bytes=64, offset=8192 * (k + 1))
             else:
-                th = work.tile([P, JH], F32, name="th")
+                th = work.tile([P, N], F32, name="th")
             nc.scalar.activation(th[:], za[:], ACT.Tanh, scale=0.5)
-            if k < ON_VECTOR:
-                sums[k] = (th, ms)
-            else:
-                eta = work.tile([P, JH], F32, name="eta")
-                nc.scalar.activation(eta[:], th[:], ACT.Copy, scale=0.5, bias=0.5)
-                ms_sb = work.tile([P, JH], F32, name="ms_sb")
-                nc.scalar.activation(ms_sb[:], ms[:], ACT.Copy)
-                sums[k] = (eta, ms_sb)
-            if k == 0:
-                own[k] = ow
-            else:
-                own[k] = work.tile([P, JH], F32, name="own_sb")
-                nc.scalar.activation(own[k][:], ow[:], ACT.Copy, scale=2.0 if k < ON_VECTOR else 1.0)
+            tanhs[k] = (th, ms)
 
         def gate(k):
-            if k == 0:
-                gated[k] = stage.tile([P, JH], F32, name="gated0", align_bytes=64, offset=4096)
-            else:
-                gated[k] = work.tile([P, JH], F32, name="gated")
-            if k < ON_VECTOR:
-                nc.vector.scalar_tensor_tensor(gated[k][:], sums[k][0][:], 1.0, sums[k][1][:], ALU.add, ALU.mult)
-            else:
-                nc.gpsimd.tensor_tensor(gated[k][:], sums[k][0][:], sums[k][1][:], ALU.mult)
+            gated[k] = work.tile([P, N], F32, name="gated")
+            nc.vector.scalar_tensor_tensor(gated[k][:], tanhs[k][0][:], 1.0, tanhs[k][1][:], ALU.add, ALU.mult)
 
-        def activate(k):
-            i, h = units[k]
-            u = work.tile([P, JH], F32, name="u")
-            if k == 0:
-                nc.vector.scalar_tensor_tensor(u[:], own[k][:], 2.0, gated[k][:], ALU.mult, ALU.add)
-            else:
-                nc.gpsimd.tensor_tensor(u[:], gated[k][:], own[k][:], ALU.add)
-            result[k] = work.tile([P, JH], F32, name="r")
-            nc.scalar.activation(
-                result[k][:], u[:], ACT.Silu, bias=bias[:, i : i + 1], scale=0.5 if k < ON_VECTOR else 1.0
+        def own_sum(k):
+            ow = psum.tile([P, N], F32, name=f"ow{k}", offset=2048 * (4 + k % 2))
+            product(ow, [("o", DST)], k)
+            own[k] = work.tile([P, N], F32, name="own")
+            nc.scalar.activation(own[k][:], ow[:], ACT.Copy, scale=2.0)
+
+        def turn(q, pair):
+            summed = psum.tile([P, 2, 2, P], F32, name=f"summed{q}{pair}", offset=2048 * (6 + pair))
+            for j in range(2):
+                for c in range(2):
+                    i = 2 * pair + c
+                    for s, term in enumerate((gated, own)):
+                        nc.tensor.matmul(
+                            summed[:, c, j, :], lhsT=term[2 * q + j][:, i * P : (i + 1) * P], rhs=identity[:],
+                            is_transpose=True, start=(s == 0), stop=(s == 1),
+                        )
+            h, first = divmod(q * JQ, JH)
+            for c in range(2):
+                i = 2 * pair + c
+                nc.scalar.activation(
+                    result[i][h][:, first : first + JQ], summed[:, c, :, :].rearrange("p j t -> p (j t)"),
+                    ACT.Silu, bias=bias[:, i : i + 1], scale=0.5,
+                )
+
+        def scatter(i, first, count):
+            h, at = divmod(first, JH)
+            nc.vector.tensor_tensor(
+                windows[i][:].indirect(dst_list[:, first // 16 : (first + count) // 16]),
+                result[i][h][:, at : at + count], edge_all[:, first : first + count], ALU.mult,
             )
-
-        def weigh(k):
-            i, h = units[k]
-            if k < last:
-                rw = work.tile([P, JH], F32, name="rw")
-                nc.gpsimd.tensor_tensor(rw[:], result[k][:], edge_w[h][:], ALU.mult)
-                result[k] = rw
-
-        def scatter(k):
-            i, h = units[k]
-            places = windows[i][:].indirect(offsets(DST, h))
-            if k < last:
-                nc.vector.tensor_copy(places, result[k][:])
-            else:
-                nc.vector.tensor_tensor(places, result[k][:], edge_w[h][:], ALU.mult)
-            if h == HALVES - 1:
+            if first + count == J:
                 nc.sync.dma_start(out[i * P : (i + 1) * P, :], windows[i][:])
 
-        cast_wo(0)
         gather_scales(0)
+        nc.sync.dma_start(wo_late[1][:], wo_rows(1, NH, NH))
+        nc.sync.dma_start(wc_w[:], wc_words.rearrange("a p x -> p a x").bitcast(I32))
+        with nc.allow_non_contiguous_dma(reason="one bias value for each partition and row tile"):
+            nc.sync.dma_start(bias[:], b.rearrange("(c p) -> p c", p=P))
+        nc.sync.dma_start(edge_all[:], wgo)
+        cast_wo()
         gather_words(0)
-        quantize_wo(0)
         gather_words(1)
-        cast_wo(1)
-        quantize_wo(1)
-        multiply(0)
-        gate(0)
-        activate(0)
-        multiply(1)
-        gate(1)
-        weigh(0)
-        activate(1)
-        gather_scales(1)
-        for k in range(2, len(units)):
-            multiply(k)
+        quantize_wo()
+        for k in range(2):
+            gate_sums(k)
+        for k in range(2):
             gate(k)
-            weigh(k - 1)
-            activate(k)
-            scatter(k - 2)
-        scatter(last - 1)
-        scatter(last)
+            own_sum(k)
+        gather_scales(1)
+        gate_sums(2)
+        gate(2)
+        for q in range(QUARTERS - 1):
+            early = q == QUARTERS - 2
+            if early:
+                gate_sums(2 * q + 3)
+                gate(2 * q + 3)
+            turn(q, 0)
+            for i in (0, 1):
+                scatter(i, q * JQ, JQ)
+            if not early:
+                gate_sums(2 * q + 3)
+                gate(2 * q + 3)
+            turn(q, 1)
+            for i in (2, 3):
+                if (q, i) != (QUARTERS - 2, NT - 1):
+                    scatter(i, q * JQ, JQ)
+            for k in (2 * q + 2, 2 * q + 3):
+                own_sum(k)
+            if 2 * q + 4 < BLOCKS:
+                gate_sums(2 * q + 4)
+                gate(2 * q + 4)
+        for pair in range(2):
+            turn(QUARTERS - 1, pair)
+        for i in range(NT - 1):
+            scatter(i, J - JQ, JQ)
+        scatter(NT - 1, J - JH, JH)

@@ -76,25 +76,25 @@ def tile_list_rgg_ownsilu_kernel(
             )
         w_s8 = w_s[:].bitcast(U8)
 
-        wo_first = keep.tile([P, 4, N], F32, name="wo_first")
-        wo_late = [
-            stage.tile([P, 4, NH], F32, name=f"wo_late{g}", offset=12288 - 4096 * g) for g in range(N // NH)
+        wo_raw = [
+            [stage.tile([P, 4, NH], F32, name=f"wo_raw{a}{g}", offset=8192 + 4096 * (3 - 2 * a - g)) for g in range(2)]
+            for a in range(PASSES)
         ]
 
-        def wo_rows(a, first, width):
-            return wo[512 * a : 512 * (a + 1), first : first + width].rearrange("(p i) n -> p i n", i=4)
+        def load_wo(a, g):
+            rows = wo[512 * a : 512 * (a + 1), g * NH : (g + 1) * NH]
+            nc.sync.dma_start(wo_raw[a][g][:], rows.rearrange("(p i) n -> p i n", i=4))
 
         wa_w = keep.tile([P, PASSES, N], I32, name="wa_w", align_bytes=64)
         wb_w = keep.tile([P, PASSES, N // 2], I32, name="wb_w", align_bytes=64)
         wc_w = keep.tile([P, PASSES, N // 2], I32, name="wc_w", align_bytes=64)
         edge_all = keep.tile([P, J], F32, name="edge_all")
         bias = keep.tile([P, NT], F32, name="bias")
-        nc.sync.dma_start(wo_first[:], wo_rows(0, 0, N))
+        load_wo(0, 0)
         nc.sync.dma_start(wa_w[:], wa_words.rearrange("a p n i -> p a (n i)").bitcast(I32))
         nc.sync.dma_start(wb_w[:], wb_words.rearrange("a p x -> p a x").bitcast(I32))
-        nc.sync.dma_start(wo_late[0][:], wo_rows(1, 0, NH))
-        for q in range(4):
-            nc.sync.dma_start(w_s[32 * q : 32 * q + 4, :], w_rows[4 * q : 4 * q + 4, :])
+        load_wo(0, 1)
+        nc.sync.dma_start(wc_w[:], wc_words.rearrange("a p x -> p a x").bitcast(I32))
 
         wo_bf = stage.tile([P, PASSES, N * 4], BF16, name="wo_bf", align_bytes=64, offset=0)
         wo_w = keep.tile([P, PASSES, N], U32, name="wo_w", align_bytes=64)
@@ -105,7 +105,7 @@ def tile_list_rgg_ownsilu_kernel(
                 for g in range(N // NH):
                     nc.scalar.activation(
                         wo_bf[:, a, 4 * NH * g : 4 * NH * (g + 1)].rearrange("p (c e i) -> p c i e", e=4, i=4),
-                        (wo_late[g][:] if a else wo_first[:, :, g * NH : (g + 1) * NH]).rearrange("p i (c e) -> p c i e", e=4),
+                        wo_raw[a][g][:].rearrange("p i (c e) -> p c i e", e=4),
                         ACT.Copy,
                     )
 
@@ -116,38 +116,45 @@ def tile_list_rgg_ownsilu_kernel(
                 in_=wo_bf[:].rearrange("p a x -> p (a x)"),
             )
 
+        got_first = keep.tile([P, 2, JH], U8, name="got_first", align_bytes=64)
         got_s = [
-            keep.tile([P, 2, JH], U8, name="got_s0", align_bytes=64),
-            stage.tile([P, 2, JH], U8, name="got_s1", align_bytes=64, offset=16384),
+            [got_first[:, l, :] for l in range(2)],
+            [stage.tile([P, JH], U8, name=f"got_s1{l}", align_bytes=64, offset=26624 - 2048 * l)[:] for l in range(2)],
         ]
-        got_w = [keep.tile([P, 2, JH], U32, name=f"got_w{h}", tag="got_w", align_bytes=64) for h in range(HALVES)]
-        parted = [keep.tile([P, 2, PASSES, 2 * JH], U8, name=f"parted{h}", align_bytes=64) for h in range(HALVES)]
+        got_w = [
+            [stage.tile([P, JH], U32, name=f"got_w{h}{l}", align_bytes=64, offset=26624 + 2048 * l) for l in range(2)]
+            for h in range(HALVES)
+        ]
+        parted = [
+            [keep.tile([P, PASSES, 2 * JH], U8, name=f"parted{h}{l}", align_bytes=64) for l in range(2)]
+            for h in range(HALVES)
+        ]
         half_words = 2 * JH // 4
 
         def offsets(l, h):
             return lists[l][:, h * (JH // 16) : (h + 1) * (JH // 16)]
 
-        def gather_scales(h):
-            for l in range(2):
-                nc.vector.tensor_copy(got_s[h][:, l, :], tab_s[:].bitcast(U8).indirect(offsets(l, h)))
-            nc.sync.dma_start(
-                shifted[0:SHIFT_ROWS, h * half_words : (h + 1) * half_words],
-                got_s[h][16:P, :, :].rearrange("p l j -> p (l j)").bitcast(I32),
-            )
+        def gather_scales(h, l):
+            nc.vector.tensor_copy(got_s[h][l], tab_s[:].bitcast(U8).indirect(offsets(l, h)))
+
+        def shift_scales(source, first):
+            words = source.bitcast(I32)
+            nc.sync.dma_start(shifted[0:SHIFT_ROWS, first : first + words.shape[1]], words[16:P, :])
 
         def gather_words(h):
             for l in range(2):
-                nc.vector.tensor_copy(got_w[h][:, l, :], tab_w[:].bitcast(U32).indirect(offsets(l, h)))
-            nc.vector.tensor_copy(
-                parted[h][:].bitcast(U16),
-                got_w[h][:].bitcast(U16).rearrange("p l (j d) -> p l d j", d=PASSES),
-            )
+                nc.vector.tensor_copy(got_w[h][l][:], tab_w[:].bitcast(U32).indirect(offsets(l, h)))
+            for l in range(2):
+                nc.vector.tensor_copy(
+                    parted[h][l][:].bitcast(U16),
+                    got_w[h][l][:].bitcast(U16).rearrange("p (j d) -> p d j", d=PASSES),
+                )
 
         def table_operand(l, block, a):
             h, first = divmod(block * P, JH)
-            codes = parted[h][:, l, a, 2 * first : 2 * (first + P)].bitcast(FP4X4)
+            codes = parted[h][l][:, a, 2 * first : 2 * (first + P)].bitcast(FP4X4)
             if a == 0:
-                return codes, got_s[h][:, l, first : first + P]
+                return codes, got_s[h][l][:, first : first + P]
             word = h * half_words + (l * JH + first) // 4
             return codes, shifted[:, word : word + P // 4].bitcast(U8)
 
@@ -162,7 +169,7 @@ def tile_list_rgg_ownsilu_kernel(
             return words[:, a, :].bitcast(FP4X4), scales
 
         def product(acc, terms, block):
-            passes = [(name, l, a) for a in range(PASSES) for name, l in terms]
+            passes = [(name, l, a) for a in reversed(range(PASSES)) for name, l in terms]
             for s, (name, l, a) in enumerate(passes):
                 w_codes, w_scales = weight_operand(name, a)
                 t_codes, t_scales = table_operand(l, block, a)
@@ -180,12 +187,12 @@ def tile_list_rgg_ownsilu_kernel(
         result = [[keep.tile([P, JH], F32, name=f"result{i}{h}") for h in range(HALVES)] for i in range(NT)]
 
         def gate_sums(k):
-            za = psum.tile([P, N], F32, name=f"za{k}", offset=2048 * (k % 2))
+            za = psum.tile([P, N], F32, name=f"za{k}", offset=2048 * (k % 2 if k % 2 or k == 0 else 4))
             ms = psum.tile([P, N], F32, name=f"ms{k}", offset=2048 * (2 + k % 2))
             product(za, [("a", DST), ("b", SRC)], k)
             product(ms, [("c", SRC)], k)
             if k < 2:
-                th = stage.tile([P, N], F32, name=f"th{k}", align_bytes=64, offset=8192 * (k + 1))
+                th = stage.tile([P, N], F32, name=f"th{k}", align_bytes=64, offset=8192 + 16384 * k)
             else:
                 th = work.tile([P, N], F32, name="th")
             nc.scalar.activation(th[:], za[:], ACT.Tanh, scale=0.5)
@@ -196,26 +203,23 @@ def tile_list_rgg_ownsilu_kernel(
             nc.vector.scalar_tensor_tensor(gated[k][:], tanhs[k][0][:], 1.0, tanhs[k][1][:], ALU.add, ALU.mult)
 
         def own_sum(k):
-            ow = psum.tile([P, N], F32, name=f"ow{k}", offset=2048 * (4 + k % 2))
+            ow = psum.tile([P, N], F32, name=f"ow{k}", offset=2048 * (k % 2))
             product(ow, [("o", DST)], k)
             own[k] = work.tile([P, N], F32, name="own")
             nc.scalar.activation(own[k][:], ow[:], ACT.Copy, scale=2.0)
 
         def turn(q, pair):
-            summed = psum.tile([P, 2, 2, P], F32, name=f"summed{q}{pair}", offset=2048 * (6 + pair))
-            for j in range(2):
-                for c in range(2):
-                    i = 2 * pair + c
+            h, first = divmod(q * JQ, JH)
+            for i in (2 * pair, 2 * pair + 1):
+                summed = psum.tile([P, 2, P], F32, name=f"summed{q}{i}", offset=2048 * (5 + (NT * q + i) % 3))
+                for j in range(2):
                     for s, term in enumerate((gated, own)):
                         nc.tensor.matmul(
-                            summed[:, c, j, :], lhsT=term[2 * q + j][:, i * P : (i + 1) * P], rhs=identity[:],
+                            summed[:, j, :], lhsT=term[2 * q + j][:, i * P : (i + 1) * P], rhs=identity[:],
                             is_transpose=True, start=(s == 0), stop=(s == 1),
                         )
-            h, first = divmod(q * JQ, JH)
-            for c in range(2):
-                i = 2 * pair + c
                 nc.scalar.activation(
-                    result[i][h][:, first : first + JQ], summed[:, c, :, :].rearrange("p j t -> p (j t)"),
+                    result[i][h][:, first : first + JQ], summed[:].rearrange("p j t -> p (j t)"),
                     ACT.Silu, bias=bias[:, i : i + 1], scale=0.5,
                 )
 
@@ -228,22 +232,29 @@ def tile_list_rgg_ownsilu_kernel(
             if first + count == J:
                 nc.sync.dma_start(out[i * P : (i + 1) * P, :], windows[i][:])
 
-        gather_scales(0)
-        nc.sync.dma_start(wo_late[1][:], wo_rows(1, NH, NH))
-        nc.sync.dma_start(wc_w[:], wc_words.rearrange("a p x -> p a x").bitcast(I32))
+        for q in range(4):
+            nc.sync.dma_start(w_s[32 * q : 32 * q + 4, :], w_rows[4 * q : 4 * q + 4, :])
+        for l in range(2):
+            gather_scales(0, l)
+        shift_scales(got_first[:].rearrange("p l j -> p (l j)"), 0)
+        load_wo(1, 0)
+        load_wo(1, 1)
         with nc.allow_non_contiguous_dma(reason="one bias value for each partition and row tile"):
             nc.sync.dma_start(bias[:], b.rearrange("(c p) -> p c", p=P))
         nc.sync.dma_start(edge_all[:], wgo)
         cast_wo()
         gather_words(0)
         gather_words(1)
+        gather_scales(1, DST)
+        shift_scales(got_s[1][DST], half_words)
         quantize_wo()
         for k in range(2):
             gate_sums(k)
         for k in range(2):
             gate(k)
             own_sum(k)
-        gather_scales(1)
+        gather_scales(1, SRC)
+        shift_scales(got_s[1][SRC], half_words + JH // 4)
         gate_sums(2)
         gate(2)
         for q in range(QUARTERS - 1):

@@ -76,10 +76,7 @@ def tile_list_rgg_ownsilu_kernel(
             )
         w_s8 = w_s[:].bitcast(U8)
 
-        wo_raw = [
-            [stage.tile([P, 4, NH], F32, name=f"wo_raw{a}{g}", offset=8192 + 4096 * (3 - 2 * a - g)) for g in range(2)]
-            for a in range(PASSES)
-        ]
+        wo_raw = [[keep.tile([P, 4, NH], F32, name=f"wo_raw{a}{g}") for g in range(2)] for a in range(PASSES)]
 
         def load_wo(a, g):
             rows = wo[512 * a : 512 * (a + 1), g * NH : (g + 1) * NH]
@@ -91,30 +88,36 @@ def tile_list_rgg_ownsilu_kernel(
         edge_all = keep.tile([P, J], F32, name="edge_all")
         bias = keep.tile([P, NT], F32, name="bias")
         load_wo(0, 0)
+        with nc.allow_non_contiguous_dma(reason="one bias value for each partition and row tile"):
+            nc.sync.dma_start(bias[:], b.rearrange("(c p) -> p c", p=P))
         nc.sync.dma_start(wa_w[:], wa_words.rearrange("a p n i -> p a (n i)").bitcast(I32))
         nc.sync.dma_start(wb_w[:], wb_words.rearrange("a p x -> p a x").bitcast(I32))
-        load_wo(0, 1)
         nc.sync.dma_start(wc_w[:], wc_words.rearrange("a p x -> p a x").bitcast(I32))
 
-        wo_bf = stage.tile([P, PASSES, N * 4], BF16, name="wo_bf", align_bytes=64, offset=0)
         wo_w = keep.tile([P, PASSES, N], U32, name="wo_w", align_bytes=64)
         wo_s = keep.tile([P, PASSES, N], U8, name="wo_s", align_bytes=64)
 
-        def cast_wo():
+        def quantize_wo(g):
+            wo_bf = keep.tile([P, PASSES, NH * 4], BF16, name="wo_bf", align_bytes=64)
             for a in range(PASSES):
-                for g in range(N // NH):
+                if g == 0:
                     nc.scalar.activation(
-                        wo_bf[:, a, 4 * NH * g : 4 * NH * (g + 1)].rearrange("p (c e i) -> p c i e", e=4, i=4),
+                        wo_bf[:, a, :].rearrange("p (c e i) -> p c i e", e=4, i=4),
                         wo_raw[a][g][:].rearrange("p i (c e) -> p c i e", e=4),
                         ACT.Copy,
                     )
-
-        def quantize_wo():
-            nc.vector.quantize_mx(
-                out=wo_w[:].rearrange("p a n -> p (a n)").bitcast(FP8X4),
-                scales=wo_s[:].rearrange("p a n -> p (a n)"),
-                in_=wo_bf[:].rearrange("p a x -> p (a x)"),
-            )
+                else:
+                    nc.gpsimd.tensor_scalar(
+                        wo_bf[:, a, :].rearrange("p (n i) -> p n i", i=4),
+                        wo_raw[a][g][:].rearrange("p i n -> p n i"),
+                        1.0, 0.0, ALU.mult, ALU.add,
+                    )
+            for a in range(PASSES):
+                nc.vector.quantize_mx(
+                    out=wo_w[:, a, g * NH : (g + 1) * NH].bitcast(FP8X4),
+                    scales=wo_s[:, a, g * NH : (g + 1) * NH],
+                    in_=wo_bf[:, a, :],
+                )
 
         got_first = keep.tile([P, 2, JH], U8, name="got_first", align_bytes=64)
         got_s = [
@@ -158,9 +161,9 @@ def tile_list_rgg_ownsilu_kernel(
             word = h * half_words + (l * JH + first) // 4
             return codes, shifted[:, word : word + P // 4].bitcast(U8)
 
-        def weight_operand(name, a):
+        def weight_operand(name, a, columns):
             if name == "o":
-                return wo_w[:, a, :].bitcast(FP8X4), wo_s[:, a, :]
+                return wo_w[:, a, columns].bitcast(FP8X4), wo_s[:, a, columns]
             first = ("abc".index(name) * PASSES + a) * N
             scales = w_s8[:, first : first + N]
             if name == "a":
@@ -168,13 +171,13 @@ def tile_list_rgg_ownsilu_kernel(
             words = wb_w if name == "b" else wc_w
             return words[:, a, :].bitcast(FP4X4), scales
 
-        def product(acc, terms, block):
+        def product(acc, terms, block, columns=slice(0, N)):
             passes = [(name, l, a) for a in reversed(range(PASSES)) for name, l in terms]
             for s, (name, l, a) in enumerate(passes):
-                w_codes, w_scales = weight_operand(name, a)
+                w_codes, w_scales = weight_operand(name, a, columns)
                 t_codes, t_scales = table_operand(l, block, a)
                 nc.tensor.matmul_mx(
-                    out=acc[:], lhsT=t_codes, lhsT_scale=t_scales, rhs=w_codes, rhs_scale=w_scales,
+                    out=acc, lhsT=t_codes, lhsT_scale=t_scales, rhs=w_codes, rhs_scale=w_scales,
                     start=(s == 0), stop=(s == len(passes) - 1),
                 )
 
@@ -189,10 +192,10 @@ def tile_list_rgg_ownsilu_kernel(
         def gate_sums(k):
             za = psum.tile([P, N], F32, name=f"za{k}", offset=2048 * (k % 2 if k % 2 or k == 0 else 4))
             ms = psum.tile([P, N], F32, name=f"ms{k}", offset=2048 * (2 + k % 2))
-            product(za, [("a", DST), ("b", SRC)], k)
-            product(ms, [("c", SRC)], k)
-            if k < 2:
-                th = stage.tile([P, N], F32, name=f"th{k}", align_bytes=64, offset=8192 + 16384 * k)
+            product(za[:], [("a", DST), ("b", SRC)], k)
+            product(ms[:], [("c", SRC)], k)
+            if k == 1:
+                th = stage.tile([P, N], F32, name="th1", align_bytes=64, offset=24576)
             else:
                 th = work.tile([P, N], F32, name="th")
             nc.scalar.activation(th[:], za[:], ACT.Tanh, scale=0.5)
@@ -204,9 +207,17 @@ def tile_list_rgg_ownsilu_kernel(
 
         def own_sum(k):
             ow = psum.tile([P, N], F32, name=f"ow{k}", offset=2048 * (k % 2))
-            product(ow, [("o", DST)], k)
+            product(ow[:], [("o", DST)], k)
             own[k] = work.tile([P, N], F32, name="own")
             nc.scalar.activation(own[k][:], ow[:], ACT.Copy, scale=2.0)
+
+        def own_half(k, g):
+            ow = psum.tile([P, NH], F32, name=f"ow{k}{g}", offset=2048 * (k % 2))
+            for c in range(NH // P):
+                product(ow[:, c * P : (c + 1) * P], [("o", DST)], k, slice(g * NH + c * P, g * NH + (c + 1) * P))
+            if g == 0:
+                own[k] = work.tile([P, N], F32, name="own")
+            nc.scalar.activation(own[k][:, g * NH : (g + 1) * NH], ow[:], ACT.Copy, scale=2.0)
 
         def turn(q, pair):
             h, first = divmod(q * JQ, JH)
@@ -238,23 +249,20 @@ def tile_list_rgg_ownsilu_kernel(
             gather_scales(0, l)
         shift_scales(got_first[:].rearrange("p l j -> p (l j)"), 0)
         load_wo(1, 0)
+        load_wo(0, 1)
         load_wo(1, 1)
-        with nc.allow_non_contiguous_dma(reason="one bias value for each partition and row tile"):
-            nc.sync.dma_start(bias[:], b.rearrange("(c p) -> p c", p=P))
         nc.sync.dma_start(edge_all[:], wgo)
-        cast_wo()
         gather_words(0)
         gather_words(1)
-        gather_scales(1, DST)
-        shift_scales(got_s[1][DST], half_words)
-        quantize_wo()
+        quantize_wo(0)
         for k in range(2):
             gate_sums(k)
-        for k in range(2):
+            own_half(k, 0)
             gate(k)
-            own_sum(k)
-        gather_scales(1, SRC)
-        shift_scales(got_s[1][SRC], half_words + JH // 4)
+        for l in range(2):
+            gather_scales(1, l)
+            shift_scales(got_s[1][l], half_words + l * (JH // 4))
+        quantize_wo(1)
         gate_sums(2)
         gate(2)
         for q in range(QUARTERS - 1):
@@ -263,6 +271,9 @@ def tile_list_rgg_ownsilu_kernel(
                 gate_sums(2 * q + 3)
                 gate(2 * q + 3)
             turn(q, 0)
+            if q == 0:
+                for k in range(2):
+                    own_half(k, 1)
             for i in (0, 1):
                 scatter(i, q * JQ, JQ)
             if not early:

@@ -45,19 +45,21 @@ def tile_list_rgg_ownsilu_kernel(
         tab_s = keep.tile([P, T // 4], I32, name="tab_s", align_bytes=64)
         w_s = keep.tile([P, 3 * PASSES * N // 4], I32, name="w_s", align_bytes=64)
         shifted = keep.tile([P, HALVES * 2 * JH // 4 + 1], I32, name="shifted", align_bytes=64)
-        windows = [keep.tile([P, T], F32, name=f"window{i}", align_bytes=64) for i in range(NT)]
+        windows = [keep.tile([P, T], F32, name=f"window{i}", align_bytes=64) for i in range(2)]
+        windows.extend(
+            stage.tile([P, T], F32, name=f"window{i}", align_bytes=64, offset=8192 * (i - 2)) for i in range(2, NT)
+        )
         warm = keep.tile([P, 1], F32, name="warm")
 
         nc.gpsimd.memset(tab_s[:], 0)
         nc.gpsimd.memset(w_s[:], 0)
         identity = keep.tile([P, P], F32, name="identity")
         make_identity(nc, identity[:])
-        for window in windows[:-1]:
-            nc.gpsimd.memset(window[:], 0.0)
+        nc.gpsimd.memset(windows[0][:], 0.0)
         nc.vector.memset(warm[:], 0.0)
         nc.vector.memset(shifted[:], 0)
-        nc.vector.memset(windows[-1][:, 0 : T // 2 - 1], 0.0)
-        nc.vector.memset(windows[-1][:, T // 2 - 1 : T], 0.0)
+        nc.vector.memset(windows[1][:, 0 : T // 2 - 1], 0.0)
+        nc.vector.memset(windows[1][:, T // 2 - 1 : T], 0.0)
         nc.scalar.activation(warm[:], warm[:], ACT.Silu)
 
         nc.sync.dma_start(dst_list[:], offs2)
@@ -76,11 +78,11 @@ def tile_list_rgg_ownsilu_kernel(
             )
         w_s8 = w_s[:].bitcast(U8)
 
-        wo_raw = [[keep.tile([P, 4, NH], F32, name=f"wo_raw{a}{g}") for g in range(2)] for a in range(PASSES)]
+        wo_raw = [[keep.tile([P, 4, NH], F32, name=f"wo_raw{a}{g}")[:] for g in range(2)] for a in range(PASSES)]
 
         def load_wo(a, g):
             rows = wo[512 * a : 512 * (a + 1), g * NH : (g + 1) * NH]
-            nc.sync.dma_start(wo_raw[a][g][:], rows.rearrange("(p i) n -> p i n", i=4))
+            nc.sync.dma_start(wo_raw[a][g], rows.rearrange("(p i) n -> p i n", i=4))
 
         wa_w = keep.tile([P, PASSES, N], I32, name="wa_w", align_bytes=64)
         wb_w = keep.tile([P, PASSES, N // 2], I32, name="wb_w", align_bytes=64)
@@ -98,19 +100,19 @@ def tile_list_rgg_ownsilu_kernel(
         wo_s = keep.tile([P, PASSES, N], U8, name="wo_s", align_bytes=64)
 
         def quantize_wo(g):
-            wo_bf = keep.tile([P, PASSES, NH * 4], BF16, name="wo_bf", align_bytes=64)
+            wo_bf = stage.tile([P, PASSES, NH * 4], BF16, name=f"wo_bf{g}", align_bytes=64, offset=6144)
             for a in range(PASSES):
-                if g == 0:
-                    nc.scalar.activation(
-                        wo_bf[:, a, :].rearrange("p (c e i) -> p c i e", e=4, i=4),
-                        wo_raw[a][g][:].rearrange("p i (c e) -> p c i e", e=4),
-                        ACT.Copy,
-                    )
-                else:
+                if (a, g) == (0, 1):
                     nc.gpsimd.tensor_scalar(
                         wo_bf[:, a, :].rearrange("p (n i) -> p n i", i=4),
-                        wo_raw[a][g][:].rearrange("p i n -> p n i"),
+                        wo_raw[a][g].rearrange("p i n -> p n i"),
                         1.0, 0.0, ALU.mult, ALU.add,
+                    )
+                else:
+                    nc.scalar.activation(
+                        wo_bf[:, a, :].rearrange("p (c e i) -> p c i e", e=4, i=4),
+                        wo_raw[a][g].rearrange("p i (c e) -> p c i e", e=4),
+                        ACT.Copy,
                     )
             for a in range(PASSES):
                 nc.vector.quantize_mx(
@@ -263,6 +265,8 @@ def tile_list_rgg_ownsilu_kernel(
             gather_scales(1, l)
             shift_scales(got_s[1][l], half_words + l * (JH // 4))
         quantize_wo(1)
+        for window in windows[2:]:
+            nc.gpsimd.memset(window[:], 0.0)
         gate_sums(2)
         gate(2)
         for q in range(QUARTERS - 1):

@@ -78,7 +78,13 @@ def tile_list_rgg_ownsilu_kernel(
             )
         w_s8 = w_s[:].bitcast(U8)
 
-        wo_raw = [[keep.tile([P, 4, NH], F32, name=f"wo_raw{a}{g}")[:] for g in range(2)] for a in range(PASSES)]
+        wo_raw = [
+            [
+                stage.tile([P, 4, NH], F32, name=f"wo_raw{a}{g}", align_bytes=64, offset=32768 + 4096 * (2 * a + g))[:]
+                for g in range(2)
+            ]
+            for a in range(PASSES)
+        ]
 
         def load_wo(a, g):
             rows = wo[512 * a : 512 * (a + 1), g * NH : (g + 1) * NH]
@@ -89,7 +95,6 @@ def tile_list_rgg_ownsilu_kernel(
         wc_w = keep.tile([P, PASSES, N // 2], I32, name="wc_w", align_bytes=64)
         edge_all = keep.tile([P, J], F32, name="edge_all")
         bias = keep.tile([P, NT], F32, name="bias")
-        load_wo(0, 0)
         with nc.allow_non_contiguous_dma(reason="one bias value for each partition and row tile"):
             nc.sync.dma_start(bias[:], b.rearrange("(c p) -> p c", p=P))
         nc.sync.dma_start(wa_w[:], wa_words.rearrange("a p n i -> p a (n i)").bitcast(I32))
@@ -100,17 +105,21 @@ def tile_list_rgg_ownsilu_kernel(
         wo_s = keep.tile([P, PASSES, N], U8, name="wo_s", align_bytes=64)
 
         def quantize_wo(g):
-            wo_bf = stage.tile([P, PASSES, NH * 4], BF16, name=f"wo_bf{g}", align_bytes=64, offset=6144)
+            places = ((6144, 8192), (0, 7168))[g]
+            wo_bf = [
+                stage.tile([P, NH * 4], BF16, name=f"wo_bf{a}{g}", align_bytes=64, offset=places[a])
+                for a in range(PASSES)
+            ]
             for a in range(PASSES):
-                if (a, g) == (0, 1):
+                if (a, g) == (1, 1):
                     nc.gpsimd.tensor_scalar(
-                        wo_bf[:, a, :].rearrange("p (n i) -> p n i", i=4),
+                        wo_bf[a][:].rearrange("p (n i) -> p n i", i=4),
                         wo_raw[a][g].rearrange("p i n -> p n i"),
                         1.0, 0.0, ALU.mult, ALU.add,
                     )
                 else:
                     nc.scalar.activation(
-                        wo_bf[:, a, :].rearrange("p (c e i) -> p c i e", e=4, i=4),
+                        wo_bf[a][:].rearrange("p (c e i) -> p c i e", e=4, i=4),
                         wo_raw[a][g].rearrange("p i (c e) -> p c i e", e=4),
                         ACT.Copy,
                     )
@@ -118,22 +127,15 @@ def tile_list_rgg_ownsilu_kernel(
                 nc.vector.quantize_mx(
                     out=wo_w[:, a, g * NH : (g + 1) * NH].bitcast(FP8X4),
                     scales=wo_s[:, a, g * NH : (g + 1) * NH],
-                    in_=wo_bf[:, a, :],
+                    in_=wo_bf[a][:],
                 )
 
         got_first = keep.tile([P, 2, JH], U8, name="got_first", align_bytes=64)
         got_s = [
             [got_first[:, l, :] for l in range(2)],
-            [stage.tile([P, JH], U8, name=f"got_s1{l}", align_bytes=64, offset=26624 - 2048 * l)[:] for l in range(2)],
+            [stage.tile([P, JH], U8, name=f"got_s1{l}", align_bytes=64, offset=(26624, 43008)[l])[:] for l in range(2)],
         ]
-        got_w = [
-            [stage.tile([P, JH], U32, name=f"got_w{h}{l}", align_bytes=64, offset=26624 + 2048 * l) for l in range(2)]
-            for h in range(HALVES)
-        ]
-        parted = [
-            [keep.tile([P, PASSES, 2 * JH], U8, name=f"parted{h}{l}", align_bytes=64) for l in range(2)]
-            for h in range(HALVES)
-        ]
+        parted = {}
         half_words = 2 * JH // 4
 
         def offsets(l, h):
@@ -146,18 +148,25 @@ def tile_list_rgg_ownsilu_kernel(
             words = source.bitcast(I32)
             nc.sync.dma_start(shifted[0:SHIFT_ROWS, first : first + words.shape[1]], words[16:P, :])
 
-        def gather_words(h):
+        def gather_words(first, count):
+            got_w = [
+                stage.tile([P, count], U32, name=f"got_w{first}_{l}", align_bytes=64, offset=26624 + 2048 * l)
+                for l in range(2)
+            ]
             for l in range(2):
-                nc.vector.tensor_copy(got_w[h][l][:], tab_w[:].bitcast(U32).indirect(offsets(l, h)))
+                picks = lists[l][:, first // 16 : (first + count) // 16]
+                nc.vector.tensor_copy(got_w[l][:], tab_w[:].bitcast(U32).indirect(picks))
             for l in range(2):
+                codes = keep.tile([P, PASSES, 2 * count], U8, name=f"parted{first}_{l}", align_bytes=64)
                 nc.vector.tensor_copy(
-                    parted[h][l][:].bitcast(U16),
-                    got_w[h][l][:].bitcast(U16).rearrange("p (j d) -> p d j", d=PASSES),
+                    codes[:].bitcast(U16), got_w[l][:].bitcast(U16).rearrange("p (j d) -> p d j", d=PASSES)
                 )
+                for at in range(0, count, P):
+                    parted[l, (first + at) // P] = codes[:, :, 2 * at : 2 * (at + P)]
 
         def table_operand(l, block, a):
             h, first = divmod(block * P, JH)
-            codes = parted[h][l][:, a, 2 * first : 2 * (first + P)].bitcast(FP4X4)
+            codes = parted[l, block][:, a, :].bitcast(FP4X4)
             if a == 0:
                 return codes, got_s[h][l][:, first : first + P]
             word = h * half_words + (l * JH + first) // 4
@@ -192,12 +201,14 @@ def tile_list_rgg_ownsilu_kernel(
         result = [[keep.tile([P, JH], F32, name=f"result{i}{h}") for h in range(HALVES)] for i in range(NT)]
 
         def gate_sums(k):
-            za = psum.tile([P, N], F32, name=f"za{k}", offset=2048 * (k % 2 if k % 2 or k == 0 else 4))
+            za = psum.tile([P, N], F32, name=f"za{k}", offset=2048 * (k % 2 if k % 2 or k <= 2 else 4))
             ms = psum.tile([P, N], F32, name=f"ms{k}", offset=2048 * (2 + k % 2))
             product(za[:], [("a", DST), ("b", SRC)], k)
             product(ms[:], [("c", SRC)], k)
-            if k == 1:
-                th = stage.tile([P, N], F32, name="th1", align_bytes=64, offset=24576)
+            if k == 0:
+                th = stage.tile([P, N], F32, name="th0", align_bytes=64, offset=32768 + 4096 * 2)
+            elif k == 1:
+                th = stage.tile([P, N], F32, name="th1", align_bytes=64, offset=32768 + 4096 * 2 + 2048)
             else:
                 th = work.tile([P, N], F32, name="th")
             nc.scalar.activation(th[:], za[:], ACT.Tanh, scale=0.5)
@@ -210,16 +221,19 @@ def tile_list_rgg_ownsilu_kernel(
         def own_sum(k):
             ow = psum.tile([P, N], F32, name=f"ow{k}", offset=2048 * (k % 2))
             product(ow[:], [("o", DST)], k)
-            own[k] = work.tile([P, N], F32, name="own")
-            nc.scalar.activation(own[k][:], ow[:], ACT.Copy, scale=2.0)
+            tile = work.tile([P, N], F32, name="own")
+            own[k] = tile[:]
+            nc.scalar.activation(own[k], ow[:], ACT.Copy, scale=2.0)
 
-        def own_half(k, g):
-            ow = psum.tile([P, NH], F32, name=f"ow{k}{g}", offset=2048 * (k % 2))
-            for c in range(NH // P):
-                product(ow[:, c * P : (c + 1) * P], [("o", DST)], k, slice(g * NH + c * P, g * NH + (c + 1) * P))
-            if g == 0:
-                own[k] = work.tile([P, N], F32, name="own")
-            nc.scalar.activation(own[k][:, g * NH : (g + 1) * NH], ow[:], ACT.Copy, scale=2.0)
+        own_first = keep.tile([P, 2, N], F32, name="own_first")
+
+        def own_half(g):
+            ow = psum.tile([P, 2, NH], F32, name=f"ow_first{g}", offset=2048 * (1 - g))
+            for k in range(2):
+                own[k] = own_first[:, k, :]
+                for c in range(NH // P):
+                    product(ow[:, k, c * P : (c + 1) * P], [("o", DST)], k, slice(g * NH + c * P, g * NH + (c + 1) * P))
+            nc.scalar.activation(own_first[:, :, g * NH : (g + 1) * NH], ow[:], ACT.Copy, scale=2.0)
 
         def turn(q, pair):
             h, first = divmod(q * JQ, JH)
@@ -250,17 +264,19 @@ def tile_list_rgg_ownsilu_kernel(
         for l in range(2):
             gather_scales(0, l)
         shift_scales(got_first[:].rearrange("p l j -> p (l j)"), 0)
+        load_wo(0, 0)
         load_wo(1, 0)
         load_wo(0, 1)
         load_wo(1, 1)
         nc.sync.dma_start(edge_all[:], wgo)
-        gather_words(0)
-        gather_words(1)
+        gather_words(0, JQ)
+        gather_words(JQ, JQ)
+        gather_words(JH, JH)
         quantize_wo(0)
         for k in range(2):
             gate_sums(k)
-            own_half(k, 0)
             gate(k)
+        own_half(0)
         for l in range(2):
             gather_scales(1, l)
             shift_scales(got_s[1][l], half_words + l * (JH // 4))
@@ -276,8 +292,7 @@ def tile_list_rgg_ownsilu_kernel(
                 gate(2 * q + 3)
             turn(q, 0)
             if q == 0:
-                for k in range(2):
-                    own_half(k, 1)
+                own_half(1)
             for i in (0, 1):
                 scatter(i, q * JQ, JQ)
             if not early:

@@ -24,6 +24,7 @@ HALVES = J // JH
 NT = N // P
 NH = 256
 SHIFT_ROWS = 112
+VECTOR_GATES = 5
 
 
 def tile_list_rgg_ownsilu_kernel(
@@ -212,11 +213,20 @@ def tile_list_rgg_ownsilu_kernel(
             else:
                 th = work.tile([P, N], F32, name="th")
             nc.scalar.activation(th[:], za[:], ACT.Tanh, scale=0.5)
-            tanhs[k] = (th, ms)
+            if k < VECTOR_GATES:
+                tanhs[k] = (th, ms)
+            else:
+                message = work.tile([P, N], F32, name="message")
+                nc.scalar.activation(th[:], th[:], ACT.Copy, bias=1.0)
+                nc.scalar.activation(message[:], ms[:], ACT.Copy)
+                tanhs[k] = (th, message)
 
         def gate(k):
             gated[k] = work.tile([P, N], F32, name="gated")
-            nc.vector.scalar_tensor_tensor(gated[k][:], tanhs[k][0][:], 1.0, tanhs[k][1][:], ALU.add, ALU.mult)
+            if k < VECTOR_GATES:
+                nc.vector.scalar_tensor_tensor(gated[k][:], tanhs[k][0][:], 1.0, tanhs[k][1][:], ALU.add, ALU.mult)
+            else:
+                nc.gpsimd.tensor_tensor(gated[k][:], tanhs[k][0][:], tanhs[k][1][:], ALU.mult)
 
         def own_sum(k):
             ow = psum.tile([P, N], F32, name=f"ow{k}", offset=2048 * (k % 2))
@@ -252,10 +262,13 @@ def tile_list_rgg_ownsilu_kernel(
 
         def scatter(i, first, count):
             h, at = divmod(first, JH)
-            nc.vector.tensor_tensor(
-                windows[i][:].indirect(dst_list[:, first // 16 : (first + count) // 16]),
-                result[i][h][:, at : at + count], edge_all[:, first : first + count], ALU.mult,
-            )
+            values = result[i][h][:, at : at + count]
+            places = windows[i][:].indirect(dst_list[:, first // 16 : (first + count) // 16])
+            if first == 0 or first + count == J:
+                nc.vector.tensor_tensor(places, values, edge_all[:, first : first + count], ALU.mult)
+            else:
+                nc.gpsimd.tensor_tensor(values, values, edge_all[:, first : first + count], ALU.mult)
+                nc.vector.tensor_copy(places, values)
             if first + count == J:
                 nc.sync.dma_start(out[i * P : (i + 1) * P, :], windows[i][:])
 
@@ -286,18 +299,13 @@ def tile_list_rgg_ownsilu_kernel(
         gate_sums(2)
         gate(2)
         for q in range(QUARTERS - 1):
-            early = q == QUARTERS - 2
-            if early:
-                gate_sums(2 * q + 3)
-                gate(2 * q + 3)
             turn(q, 0)
             if q == 0:
                 own_half(1)
             for i in (0, 1):
                 scatter(i, q * JQ, JQ)
-            if not early:
-                gate_sums(2 * q + 3)
-                gate(2 * q + 3)
+            gate_sums(2 * q + 3)
+            gate(2 * q + 3)
             turn(q, 1)
             for i in (2, 3):
                 if (q, i) != (QUARTERS - 2, NT - 1):

@@ -20,11 +20,20 @@ ALU = mybir.AluOpType
 P = 128
 PASSES = 2
 JH = 512
-HALVES = J // JH
 NT = N // P
 NH = 256
+JQ = 2 * P
+BLOCKS = J // P
+QUARTERS = BLOCKS // 2
 SHIFT_ROWS = 112
-VECTOR_GATES = 5
+VECTOR_GATES = 2
+SCALAR_ONES = (4, 5, 6, 7)
+GOT = 8192
+ROUNDED = 24576
+RAW = 32768
+FIRST_BANKS = {"za0": 1, "za1": 4, "ms0": 2, "ms1": 3, "ow_first0": 4, "ow_first1": 4}
+SUM_BANKS = 5
+TURN_BANKS = 3
 
 
 def tile_list_rgg_ownsilu_kernel(
@@ -33,7 +42,6 @@ def tile_list_rgg_ownsilu_kernel(
     nc = tc.nc
     with ExitStack() as ctx:
         keep = ctx.enter_context(tc.tile_pool(name="keep", bufs=1))
-        work = ctx.enter_context(tc.tile_pool(name="work", bufs=4))
         stage = ctx.enter_context(tc.tile_pool(name="stage", bufs=1))
         psum = ctx.enter_context(tc.psum_pool(name="psum", bufs=1))
 
@@ -45,43 +53,48 @@ def tile_list_rgg_ownsilu_kernel(
         tab_w = keep.tile([P, T], I32, name="tab_w", align_bytes=64)
         tab_s = keep.tile([P, T // 4], I32, name="tab_s", align_bytes=64)
         w_s = keep.tile([P, 3 * PASSES * N // 4], I32, name="w_s", align_bytes=64)
-        shifted = keep.tile([P, HALVES * 2 * JH // 4 + 1], I32, name="shifted", align_bytes=64)
-        windows = [keep.tile([P, T], F32, name=f"window{i}", align_bytes=64) for i in range(2)]
-        windows.extend(
-            stage.tile([P, T], F32, name=f"window{i}", align_bytes=64, offset=8192 * (i - 2)) for i in range(2, NT)
-        )
+        shifted = keep.tile([P, 2 * J // 4], I32, name="shifted", align_bytes=64)
+        windows = [keep.tile([P, T], F32, name=f"window{i}", align_bytes=64) for i in range(NT - 1)]
         warm = keep.tile([P, 1], F32, name="warm")
 
-        nc.gpsimd.memset(tab_s[:], 0)
+        nc.vector.memset(tab_s[:], 0)
         nc.gpsimd.memset(w_s[:], 0)
         identity = keep.tile([P, P], F32, name="identity")
         make_identity(nc, identity[:])
         nc.gpsimd.memset(windows[0][:], 0.0)
         nc.vector.memset(warm[:], 0.0)
-        nc.vector.memset(shifted[:], 0)
-        nc.vector.memset(windows[1][:, 0 : T // 2 - 1], 0.0)
-        nc.vector.memset(windows[1][:, T // 2 - 1 : T], 0.0)
+        nc.vector.memset(shifted[:, 0:255], 0)
+        nc.vector.memset(shifted[:, 255:512], 0)
+        nc.vector.memset(windows[1][:, 0:767], 0.0)
+        nc.vector.memset(windows[1][:, 767:1536], 0.0)
+        nc.gpsimd.memset(windows[1][:, 1536:T], 0.0)
+        nc.gpsimd.memset(windows[2][:, 0 : T // 2], 0.0)
+        nc.gpsimd.memset(windows[2][:, T // 2 : T], 0.0)
         nc.scalar.activation(warm[:], warm[:], ACT.Silu)
 
         nc.sync.dma_start(dst_list[:], offs2)
-        nc.sync.dma_start(src_list[:], offs)
         for r in range(4):
             nc.sync.dma_start(
                 tab_s[r:P:16, :], tab_scales.bitcast(I32).rearrange("a (q r) t -> r q a t", r=4)[r]
             )
-        nc.sync.dma_start(tab_w[:], tab_words[0].rearrange("p t b -> p (t b)").bitcast(I32))
+        nc.sync.dma_start(src_list[:], offs)
         row_words = PASSES * N // 4
-        w_rows = keep.tile([16, 3 * row_words], I32, name="w_rows")
-        for w, scales in enumerate((wa_scales, wb_scales, wc_scales)):
+
+        def load_rows(w, scales):
             nc.sync.dma_start(
-                w_rows[:, w * row_words : (w + 1) * row_words].rearrange("q (a n) -> q a n", a=PASSES),
+                w_s[0:P:8, w * row_words : (w + 1) * row_words].rearrange("q (a n) -> q a n", a=PASSES),
                 scales.bitcast(I32).rearrange("a q n -> q a n"),
             )
+
+        load_rows(0, wa_scales)
+        nc.sync.dma_start(tab_w[:], tab_words[0].rearrange("p t b -> p (t b)").bitcast(I32))
+        load_rows(1, wb_scales)
+        load_rows(2, wc_scales)
         w_s8 = w_s[:].bitcast(U8)
 
         wo_raw = [
             [
-                stage.tile([P, 4, NH], F32, name=f"wo_raw{a}{g}", align_bytes=64, offset=32768 + 4096 * (2 * a + g))[:]
+                stage.tile([P, 4, NH], F32, name=f"wo_raw{a}{g}", align_bytes=64, offset=RAW + 4096 * (2 * a + g))[:]
                 for g in range(2)
             ]
             for a in range(PASSES)
@@ -96,17 +109,18 @@ def tile_list_rgg_ownsilu_kernel(
         wc_w = keep.tile([P, PASSES, N // 2], I32, name="wc_w", align_bytes=64)
         edge_all = keep.tile([P, J], F32, name="edge_all")
         bias = keep.tile([P, NT], F32, name="bias")
-        with nc.allow_non_contiguous_dma(reason="one bias value for each partition and row tile"):
-            nc.sync.dma_start(bias[:], b.rearrange("(c p) -> p c", p=P))
         nc.sync.dma_start(wa_w[:], wa_words.rearrange("a p n i -> p a (n i)").bitcast(I32))
         nc.sync.dma_start(wb_w[:], wb_words.rearrange("a p x -> p a x").bitcast(I32))
         nc.sync.dma_start(wc_w[:], wc_words.rearrange("a p x -> p a x").bitcast(I32))
+        for r in range(1, 4):
+            nc.sync.dma_start(w_s[r:P:32, :], w_s[8 * r : P : 32, :])
+        load_wo(0, 0)
 
         wo_w = keep.tile([P, PASSES, N], U32, name="wo_w", align_bytes=64)
         wo_s = keep.tile([P, PASSES, N], U8, name="wo_s", align_bytes=64)
 
         def quantize_wo(g):
-            places = ((6144, 8192), (0, 7168))[g]
+            places = ((ROUNDED, ROUNDED + 2048), (ROUNDED + 4096, ROUNDED + 1024))[g]
             wo_bf = [
                 stage.tile([P, NH * 4], BF16, name=f"wo_bf{a}{g}", align_bytes=64, offset=places[a])
                 for a in range(PASSES)
@@ -131,47 +145,48 @@ def tile_list_rgg_ownsilu_kernel(
                     in_=wo_bf[a][:],
                 )
 
-        got_first = keep.tile([P, 2, JH], U8, name="got_first", align_bytes=64)
-        got_s = [
-            [got_first[:, l, :] for l in range(2)],
-            [stage.tile([P, JH], U8, name=f"got_s1{l}", align_bytes=64, offset=(26624, 43008)[l])[:] for l in range(2)],
-        ]
+        got_early = keep.tile([P, 2 * JH], U8, name="got_early", align_bytes=64)
         parted = {}
-        half_words = 2 * JH // 4
+        planes = {}
 
-        def offsets(l, h):
-            return lists[l][:, h * (JH // 16) : (h + 1) * (JH // 16)]
+        def gather_scales(target, l, first, count):
+            picks = lists[l][:, first // 16 : (first + count) // 16]
+            nc.vector.tensor_copy(target, tab_s[:].bitcast(U8).indirect(picks))
+            for at in range(0, count, P):
+                planes[l, (first + at) // P, 0] = target[:, at : at + P]
 
-        def gather_scales(h, l):
-            nc.vector.tensor_copy(got_s[h][l], tab_s[:].bitcast(U8).indirect(offsets(l, h)))
-
-        def shift_scales(source, first):
+        def shift_scales(queue, source, first):
             words = source.bitcast(I32)
-            nc.sync.dma_start(shifted[0:SHIFT_ROWS, first : first + words.shape[1]], words[16:P, :])
+            queue.dma_start(shifted[0:SHIFT_ROWS, first : first + words.shape[1]], words[16:P, :])
 
-        def gather_words(first, count):
+        for block in range(BLOCKS):
+            for l in range(2):
+                word = (block * P // JH * J + l * JH + block * P % JH) // 4
+                planes[l, block, 1] = shifted[:, word : word + P // 4].bitcast(U8)
+
+        def gather_words(first, count, places):
             got_w = [
-                stage.tile([P, count], U32, name=f"got_w{first}_{l}", align_bytes=64, offset=26624 + 2048 * l)
+                stage.tile([P, count], U32, name=f"got_w{first}_{l}", align_bytes=64, offset=places[l])
                 for l in range(2)
             ]
             for l in range(2):
                 picks = lists[l][:, first // 16 : (first + count) // 16]
                 nc.vector.tensor_copy(got_w[l][:], tab_w[:].bitcast(U32).indirect(picks))
+            return got_w
+
+        def part_words(got_w, origin, first, count, places=None):
             for l in range(2):
-                codes = keep.tile([P, PASSES, 2 * count], U8, name=f"parted{first}_{l}", align_bytes=64)
+                shape, name = [P, PASSES, 2 * count], f"parted{first}_{l}"
+                if places is None:
+                    codes = keep.tile(shape, U8, name=name, align_bytes=64)
+                else:
+                    codes = stage.tile(shape, U8, name=name, align_bytes=64, offset=places[l])
+                words = got_w[l][:, first - origin : first - origin + count]
                 nc.vector.tensor_copy(
-                    codes[:].bitcast(U16), got_w[l][:].bitcast(U16).rearrange("p (j d) -> p d j", d=PASSES)
+                    codes[:].bitcast(U16), words.bitcast(U16).rearrange("p (j d) -> p d j", d=PASSES)
                 )
                 for at in range(0, count, P):
                     parted[l, (first + at) // P] = codes[:, :, 2 * at : 2 * (at + P)]
-
-        def table_operand(l, block, a):
-            h, first = divmod(block * P, JH)
-            codes = parted[l, block][:, a, :].bitcast(FP4X4)
-            if a == 0:
-                return codes, got_s[h][l][:, first : first + P]
-            word = h * half_words + (l * JH + first) // 4
-            return codes, shifted[:, word : word + P // 4].bitcast(U8)
 
         def weight_operand(name, a, columns):
             if name == "o":
@@ -184,63 +199,71 @@ def tile_list_rgg_ownsilu_kernel(
             return words[:, a, :].bitcast(FP4X4), scales
 
         def product(acc, terms, block, columns=slice(0, N)):
-            passes = [(name, l, a) for a in reversed(range(PASSES)) for name, l in terms]
+            order = (0, 1) if block < 2 and terms[0][0] != "o" else (1, 0)
+            passes = [(name, l, a) for a in order for name, l in terms]
             for s, (name, l, a) in enumerate(passes):
                 w_codes, w_scales = weight_operand(name, a, columns)
-                t_codes, t_scales = table_operand(l, block, a)
                 nc.tensor.matmul_mx(
-                    out=acc, lhsT=t_codes, lhsT_scale=t_scales, rhs=w_codes, rhs_scale=w_scales,
-                    start=(s == 0), stop=(s == len(passes) - 1),
+                    out=acc, lhsT=parted[l, block][:, a, :].bitcast(FP4X4), lhsT_scale=planes[l, block, a],
+                    rhs=w_codes, rhs_scale=w_scales, start=(s == 0), stop=(s == len(passes) - 1),
                 )
 
-        BLOCKS = J // P
-        QUARTERS = BLOCKS // 2
-        JQ = 2 * P
-        tanhs = {}
-        gated = {}
-        own = {}
-        result = [[keep.tile([P, JH], F32, name=f"result{i}{h}") for h in range(HALVES)] for i in range(NT)]
+        addends = {k: [] for k in range(BLOCKS)}
+        factors = {}
+        result = [[keep.tile([P, JH], F32, name=f"result{i}{h}") for h in range(2)] for i in range(NT)]
+        sums_made = []
+
+        def sum_bank(name, shape):
+            bank = FIRST_BANKS.get(name)
+            if bank is None:
+                bank = len(sums_made) % SUM_BANKS
+                sums_made.append(name)
+            return psum.tile(shape, F32, name=name, offset=2048 * bank)
 
         def gate_sums(k):
-            za = psum.tile([P, N], F32, name=f"za{k}", offset=2048 * (k % 2 if k % 2 or k <= 2 else 4))
-            ms = psum.tile([P, N], F32, name=f"ms{k}", offset=2048 * (2 + k % 2))
+            za = sum_bank(f"za{k}", [P, N])
+            ms = sum_bank(f"ms{k}", [P, N])
             product(za[:], [("a", DST), ("b", SRC)], k)
             product(ms[:], [("c", SRC)], k)
-            if k == 0:
-                th = stage.tile([P, N], F32, name="th0", align_bytes=64, offset=32768 + 4096 * 2)
-            elif k == 1:
-                th = stage.tile([P, N], F32, name="th1", align_bytes=64, offset=32768 + 4096 * 2 + 2048)
+            if k < 2:
+                th = stage.tile([P, N], F32, name=f"th{k}", align_bytes=64, offset=RAW + 4096 * 2 + 2048 * k)
             else:
-                th = work.tile([P, N], F32, name="th")
+                th = keep.tile([P, N], F32, name=f"th{k}")
             nc.scalar.activation(th[:], za[:], ACT.Tanh, scale=0.5)
             if k < VECTOR_GATES:
-                tanhs[k] = (th, ms)
+                factors[k] = (th, ms)
             else:
-                message = work.tile([P, N], F32, name="message")
-                nc.scalar.activation(th[:], th[:], ACT.Copy, bias=1.0)
+                message = keep.tile([P, N], F32, name=f"message{k}")
                 nc.scalar.activation(message[:], ms[:], ACT.Copy)
-                tanhs[k] = (th, message)
+                factors[k] = (th, message)
+                if k in SCALAR_ONES:
+                    nc.scalar.activation(th[:], th[:], ACT.Copy, bias=1.0)
+                else:
+                    addends[k].append(message[:])
 
         def gate(k):
-            gated[k] = work.tile([P, N], F32, name="gated")
+            gated = keep.tile([P, N], F32, name=f"gated{k}")
+            th, message = factors[k]
             if k < VECTOR_GATES:
-                nc.vector.scalar_tensor_tensor(gated[k][:], tanhs[k][0][:], 1.0, tanhs[k][1][:], ALU.add, ALU.mult)
+                nc.vector.scalar_tensor_tensor(gated[:], th[:], 1.0, message[:], ALU.add, ALU.mult)
             else:
-                nc.gpsimd.tensor_tensor(gated[k][:], tanhs[k][0][:], tanhs[k][1][:], ALU.mult)
+                nc.gpsimd.tensor_tensor(gated[:], th[:], message[:], ALU.mult)
+            addends[k].append(gated[:])
 
         def own_sum(k):
-            ow = psum.tile([P, N], F32, name=f"ow{k}", offset=2048 * (k % 2))
+            ow = sum_bank(f"ow{k}", [P, N])
             product(ow[:], [("o", DST)], k)
-            tile = work.tile([P, N], F32, name="own")
-            own[k] = tile[:]
-            nc.scalar.activation(own[k], ow[:], ACT.Copy, scale=2.0)
+            own = keep.tile([P, N], F32, name=f"own{k}")
+            addends[k].insert(0, own[:])
+            nc.scalar.activation(own[:], ow[:], ACT.Copy, scale=2.0)
 
         own_first = keep.tile([P, 2, N], F32, name="own_first")
+        for k in range(2):
+            addends[k].append(own_first[:, k, :])
 
         def own_half(g):
-            ow = psum.tile([P, 2, NH], F32, name=f"ow_first{g}", offset=2048 * (1 - g))
+            ow = sum_bank(f"ow_first{g}", [P, 2, NH])
             for k in range(2):
-                own[k] = own_first[:, k, :]
                 for c in range(NH // P):
                     product(ow[:, k, c * P : (c + 1) * P], [("o", DST)], k, slice(g * NH + c * P, g * NH + (c + 1) * P))
             nc.scalar.activation(own_first[:, :, g * NH : (g + 1) * NH], ow[:], ACT.Copy, scale=2.0)
@@ -248,12 +271,15 @@ def tile_list_rgg_ownsilu_kernel(
         def turn(q, pair):
             h, first = divmod(q * JQ, JH)
             for i in (2 * pair, 2 * pair + 1):
-                summed = psum.tile([P, 2, P], F32, name=f"summed{q}{i}", offset=2048 * (5 + (NT * q + i) % 3))
+                summed = psum.tile(
+                    [P, 2, P], F32, name=f"summed{q}{i}", offset=2048 * (SUM_BANKS + (NT * q + i) % TURN_BANKS)
+                )
                 for j in range(2):
-                    for s, term in enumerate((gated, own)):
+                    terms = addends[2 * q + j]
+                    for s, term in enumerate(terms):
                         nc.tensor.matmul(
-                            summed[:, j, :], lhsT=term[2 * q + j][:, i * P : (i + 1) * P], rhs=identity[:],
-                            is_transpose=True, start=(s == 0), stop=(s == 1),
+                            summed[:, j, :], lhsT=term[:, i * P : (i + 1) * P], rhs=identity[:],
+                            is_transpose=True, start=(s == 0), stop=(s == len(terms) - 1),
                         )
                 nc.scalar.activation(
                     result[i][h][:, first : first + JQ], summed[:].rearrange("p j t -> p (j t)"),
@@ -264,57 +290,62 @@ def tile_list_rgg_ownsilu_kernel(
             h, at = divmod(first, JH)
             values = result[i][h][:, at : at + count]
             places = windows[i][:].indirect(dst_list[:, first // 16 : (first + count) // 16])
-            if first == 0 or first + count == J:
+            if first + count == J:
                 nc.vector.tensor_tensor(places, values, edge_all[:, first : first + count], ALU.mult)
+                nc.sync.dma_start(out[i * P : (i + 1) * P, :], windows[i][:])
             else:
                 nc.gpsimd.tensor_tensor(values, values, edge_all[:, first : first + count], ALU.mult)
                 nc.vector.tensor_copy(places, values)
-            if first + count == J:
-                nc.sync.dma_start(out[i * P : (i + 1) * P, :], windows[i][:])
 
-        for q in range(4):
-            nc.sync.dma_start(w_s[32 * q : 32 * q + 4, :], w_rows[4 * q : 4 * q + 4, :])
         for l in range(2):
-            gather_scales(0, l)
-        shift_scales(got_first[:].rearrange("p l j -> p (l j)"), 0)
-        load_wo(0, 0)
+            gather_scales(got_early[:, l * JH : (l + 1) * JH], l, 0, JH)
+        shift_scales(nc.sync, got_early[:], 0)
         load_wo(1, 0)
         load_wo(0, 1)
         load_wo(1, 1)
+        with nc.allow_non_contiguous_dma(reason="one bias value for each partition and row tile"):
+            nc.sync.dma_start(bias[:], b.rearrange("(c p) -> p c", p=P))
         nc.sync.dma_start(edge_all[:], wgo)
-        gather_words(0, JQ)
-        gather_words(JQ, JQ)
-        gather_words(JH, JH)
+        part_words(gather_words(0, JQ, (GOT + 2560, 0)), 0, 0, JQ)
+        windows.append(stage.tile([P, T], F32, name="window3", align_bytes=64, offset=0))
+        nc.gpsimd.memset(windows[3][:], 0.0)
+        rest = gather_words(JQ, J - JQ, (GOT, GOT + 3072))
+        part_words(rest, JQ, JQ, JQ)
+        part_words(rest, JQ, JH, JH)
         quantize_wo(0)
         for k in range(2):
             gate_sums(k)
             gate(k)
         own_half(0)
+        turn(0, 0)
         for l in range(2):
-            gather_scales(1, l)
-            shift_scales(got_s[1][l], half_words + l * (JH // 4))
-        quantize_wo(1)
-        for window in windows[2:]:
-            nc.gpsimd.memset(window[:], 0.0)
-        gate_sums(2)
-        gate(2)
-        for q in range(QUARTERS - 1):
-            turn(q, 0)
-            if q == 0:
-                own_half(1)
-            for i in (0, 1):
-                scatter(i, q * JQ, JQ)
-            gate_sums(2 * q + 3)
-            gate(2 * q + 3)
-            turn(q, 1)
-            for i in (2, 3):
-                if (q, i) != (QUARTERS - 2, NT - 1):
-                    scatter(i, q * JQ, JQ)
+            if l == SRC:
+                quantize_wo(1)
+            place = (RAW + 4096 * 2 + 2048, ROUNDED + 1024)[l]
+            got_late = stage.tile([P, JH], U8, name=f"got_late{l}", align_bytes=64, offset=place)
+            gather_scales(got_late[:], l, JH, JH)
+            shift_scales(nc.sync, got_late[:], (J + l * JH) // 4)
+        for i in (0, 1):
+            scatter(i, 0, JQ)
+        own_half(1)
+        turn(0, 1)
+        for i in (2, 3):
+            scatter(i, 0, JQ)
+        for k in (2, 3):
+            gate_sums(k)
+            gate(k)
+        for k in (2, 3):
+            own_sum(k)
+        for q in range(1, QUARTERS - 1):
+            for pair in range(2):
+                gate_sums(2 * q + 2 + pair)
+                turn(q, pair)
+                for i in (2 * pair, 2 * pair + 1):
+                    if (q, i) != (QUARTERS - 2, NT - 1):
+                        scatter(i, q * JQ, JQ)
+                gate(2 * q + 2 + pair)
             for k in (2 * q + 2, 2 * q + 3):
                 own_sum(k)
-            if 2 * q + 4 < BLOCKS:
-                gate_sums(2 * q + 4)
-                gate(2 * q + 4)
         for pair in range(2):
             turn(QUARTERS - 1, pair)
         for i in range(NT - 1):

@@ -26,12 +26,11 @@ JQ = 2 * P
 BLOCKS = J // P
 QUARTERS = BLOCKS // 2
 SHIFT_ROWS = 112
-VECTOR_GATES = 2
-SCALAR_ONES = (4, 5, 6, 7)
+VECTOR_GATES = 5
+SCALAR_ONES = (5, 6, 7)
 GOT = 8192
 ROUNDED = 24576
 RAW = 32768
-FIRST_BANKS = {"za0": 1, "za1": 4, "ms0": 2, "ms1": 3, "ow_first0": 4, "ow_first1": 4}
 SUM_BANKS = 5
 TURN_BANKS = 3
 
@@ -211,18 +210,10 @@ def tile_list_rgg_ownsilu_kernel(
         addends = {k: [] for k in range(BLOCKS)}
         factors = {}
         result = [[keep.tile([P, JH], F32, name=f"result{i}{h}") for h in range(2)] for i in range(NT)]
-        sums_made = []
-
-        def sum_bank(name, shape):
-            bank = FIRST_BANKS.get(name)
-            if bank is None:
-                bank = len(sums_made) % SUM_BANKS
-                sums_made.append(name)
-            return psum.tile(shape, F32, name=name, offset=2048 * bank)
 
         def gate_sums(k):
-            za = sum_bank(f"za{k}", [P, N])
-            ms = sum_bank(f"ms{k}", [P, N])
+            za = psum.tile([P, N], F32, name=f"za{k}", offset=2048 * (k % 2 if k % 2 or k <= 2 else 4))
+            ms = psum.tile([P, N], F32, name=f"ms{k}", offset=2048 * (2 + k % 2))
             product(za[:], [("a", DST), ("b", SRC)], k)
             product(ms[:], [("c", SRC)], k)
             if k < 2:
@@ -251,7 +242,7 @@ def tile_list_rgg_ownsilu_kernel(
             addends[k].append(gated[:])
 
         def own_sum(k):
-            ow = sum_bank(f"ow{k}", [P, N])
+            ow = psum.tile([P, N], F32, name=f"ow{k}", offset=2048 * (k % 2))
             product(ow[:], [("o", DST)], k)
             own = keep.tile([P, N], F32, name=f"own{k}")
             addends[k].insert(0, own[:])
@@ -262,7 +253,7 @@ def tile_list_rgg_ownsilu_kernel(
             addends[k].append(own_first[:, k, :])
 
         def own_half(g):
-            ow = sum_bank(f"ow_first{g}", [P, 2, NH])
+            ow = psum.tile([P, 2, NH], F32, name=f"ow_first{g}", offset=2048 * (1 - g))
             for k in range(2):
                 for c in range(NH // P):
                     product(ow[:, k, c * P : (c + 1) * P], [("o", DST)], k, slice(g * NH + c * P, g * NH + (c + 1) * P))
@@ -290,12 +281,13 @@ def tile_list_rgg_ownsilu_kernel(
             h, at = divmod(first, JH)
             values = result[i][h][:, at : at + count]
             places = windows[i][:].indirect(dst_list[:, first // 16 : (first + count) // 16])
-            if first + count == J:
+            if first == 0 or first + count == J:
                 nc.vector.tensor_tensor(places, values, edge_all[:, first : first + count], ALU.mult)
-                nc.sync.dma_start(out[i * P : (i + 1) * P, :], windows[i][:])
             else:
                 nc.gpsimd.tensor_tensor(values, values, edge_all[:, first : first + count], ALU.mult)
                 nc.vector.tensor_copy(places, values)
+            if first + count == J:
+                nc.sync.dma_start(out[i * P : (i + 1) * P, :], windows[i][:])
 
         for l in range(2):
             gather_scales(got_early[:, l * JH : (l + 1) * JH], l, 0, JH)
@@ -317,7 +309,6 @@ def tile_list_rgg_ownsilu_kernel(
             gate_sums(k)
             gate(k)
         own_half(0)
-        turn(0, 0)
         for l in range(2):
             if l == SRC:
                 quantize_wo(1)
@@ -325,27 +316,25 @@ def tile_list_rgg_ownsilu_kernel(
             got_late = stage.tile([P, JH], U8, name=f"got_late{l}", align_bytes=64, offset=place)
             gather_scales(got_late[:], l, JH, JH)
             shift_scales(nc.sync, got_late[:], (J + l * JH) // 4)
-        for i in (0, 1):
-            scatter(i, 0, JQ)
-        own_half(1)
-        turn(0, 1)
-        for i in (2, 3):
-            scatter(i, 0, JQ)
-        for k in (2, 3):
-            gate_sums(k)
-            gate(k)
-        for k in (2, 3):
-            own_sum(k)
-        for q in range(1, QUARTERS - 1):
-            for pair in range(2):
-                gate_sums(2 * q + 2 + pair)
-                turn(q, pair)
-                for i in (2 * pair, 2 * pair + 1):
-                    if (q, i) != (QUARTERS - 2, NT - 1):
-                        scatter(i, q * JQ, JQ)
-                gate(2 * q + 2 + pair)
+        gate_sums(2)
+        gate(2)
+        for q in range(QUARTERS - 1):
+            turn(q, 0)
+            if q == 0:
+                own_half(1)
+            for i in (0, 1):
+                scatter(i, q * JQ, JQ)
+            gate_sums(2 * q + 3)
+            gate(2 * q + 3)
+            turn(q, 1)
+            for i in (2, 3):
+                if (q, i) != (QUARTERS - 2, NT - 1):
+                    scatter(i, q * JQ, JQ)
             for k in (2 * q + 2, 2 * q + 3):
                 own_sum(k)
+            if 2 * q + 4 < BLOCKS:
+                gate_sums(2 * q + 4)
+                gate(2 * q + 4)
         for pair in range(2):
             turn(QUARTERS - 1, pair)
         for i in range(NT - 1):

@@ -28,8 +28,8 @@ QUARTERS = BLOCKS // 2
 SHIFT_ROWS = 112
 VECTOR_GATES = 5
 SCALAR_ONES = (5, 6, 7)
-GOT = 8192
-ROUNDED = 24576
+GOT = 16384
+GPSIMD_CLEARS = 1472
 RAW = 32768
 SUM_BANKS = 5
 TURN_BANKS = 3
@@ -53,22 +53,19 @@ def tile_list_rgg_ownsilu_kernel(
         tab_s = keep.tile([P, T // 4], I32, name="tab_s", align_bytes=64)
         w_s = keep.tile([P, 3 * PASSES * N // 4], I32, name="w_s", align_bytes=64)
         shifted = keep.tile([P, 2 * J // 4], I32, name="shifted", align_bytes=64)
-        windows = [keep.tile([P, T], F32, name=f"window{i}", align_bytes=64) for i in range(NT - 1)]
+        windows = [keep.tile([P, T], F32, name=f"window{i}", align_bytes=64) for i in range(2)]
         warm = keep.tile([P, 1], F32, name="warm")
 
-        nc.vector.memset(tab_s[:], 0)
+        nc.gpsimd.memset(tab_s[:], 0)
         nc.gpsimd.memset(w_s[:], 0)
         identity = keep.tile([P, P], F32, name="identity")
         make_identity(nc, identity[:])
-        nc.gpsimd.memset(windows[0][:], 0.0)
+        nc.gpsimd.memset(windows[0][:, 0:GPSIMD_CLEARS], 0.0)
         nc.vector.memset(warm[:], 0.0)
-        nc.vector.memset(shifted[:, 0:255], 0)
-        nc.vector.memset(shifted[:, 255:512], 0)
-        nc.vector.memset(windows[1][:, 0:767], 0.0)
-        nc.vector.memset(windows[1][:, 767:1536], 0.0)
-        nc.gpsimd.memset(windows[1][:, 1536:T], 0.0)
-        nc.gpsimd.memset(windows[2][:, 0 : T // 2], 0.0)
-        nc.gpsimd.memset(windows[2][:, T // 2 : T], 0.0)
+        for tile, first, last in ((shifted, 0, 2 * J // 4), (windows[1], 0, T), (windows[0], GPSIMD_CLEARS, T)):
+            middle = (first + last) // 2 - 1
+            nc.vector.memset(tile[:, first:middle], 0)
+            nc.vector.memset(tile[:, middle:last], 0)
         nc.scalar.activation(warm[:], warm[:], ACT.Silu)
 
         nc.sync.dma_start(dst_list[:], offs2)
@@ -119,24 +116,25 @@ def tile_list_rgg_ownsilu_kernel(
         wo_s = keep.tile([P, PASSES, N], U8, name="wo_s", align_bytes=64)
 
         def quantize_wo(g):
-            places = ((ROUNDED, ROUNDED + 2048), (ROUNDED + 4096, ROUNDED + 1024))[g]
+            places = ((6144, 8192), (0, 7168))[g]
             wo_bf = [
                 stage.tile([P, NH * 4], BF16, name=f"wo_bf{a}{g}", align_bytes=64, offset=places[a])
                 for a in range(PASSES)
             ]
             for a in range(PASSES):
+                first = 0
                 if (a, g) == (1, 1):
+                    first = NH // 2
                     nc.gpsimd.tensor_scalar(
-                        wo_bf[a][:].rearrange("p (n i) -> p n i", i=4),
-                        wo_raw[a][g].rearrange("p i n -> p n i"),
+                        wo_bf[a][:, 0 : 4 * first].rearrange("p (n i) -> p n i", i=4),
+                        wo_raw[a][g][:, :, 0:first].rearrange("p i n -> p n i"),
                         1.0, 0.0, ALU.mult, ALU.add,
                     )
-                else:
-                    nc.scalar.activation(
-                        wo_bf[a][:].rearrange("p (c e i) -> p c i e", e=4, i=4),
-                        wo_raw[a][g].rearrange("p i (c e) -> p c i e", e=4),
-                        ACT.Copy,
-                    )
+                nc.scalar.activation(
+                    wo_bf[a][:, 4 * first :].rearrange("p (c e i) -> p c i e", e=4, i=4),
+                    wo_raw[a][g][:, :, first:].rearrange("p i (c e) -> p c i e", e=4),
+                    ACT.Copy,
+                )
             for a in range(PASSES):
                 nc.vector.quantize_mx(
                     out=wo_w[:, a, g * NH : (g + 1) * NH].bitcast(FP8X4),
@@ -298,9 +296,7 @@ def tile_list_rgg_ownsilu_kernel(
         with nc.allow_non_contiguous_dma(reason="one bias value for each partition and row tile"):
             nc.sync.dma_start(bias[:], b.rearrange("(c p) -> p c", p=P))
         nc.sync.dma_start(edge_all[:], wgo)
-        part_words(gather_words(0, JQ, (GOT + 2560, 0)), 0, 0, JQ)
-        windows.append(stage.tile([P, T], F32, name="window3", align_bytes=64, offset=0))
-        nc.gpsimd.memset(windows[3][:], 0.0)
+        part_words(gather_words(0, JQ, (GOT + 2560, GOT + 6144)), 0, 0, JQ)
         rest = gather_words(JQ, J - JQ, (GOT, GOT + 3072))
         part_words(rest, JQ, JQ, JQ)
         part_words(rest, JQ, JH, JH)
@@ -310,12 +306,14 @@ def tile_list_rgg_ownsilu_kernel(
             gate(k)
         own_half(0)
         for l in range(2):
-            if l == SRC:
-                quantize_wo(1)
-            place = (RAW + 4096 * 2 + 2048, ROUNDED + 1024)[l]
+            place = (GOT, RAW + 4096 * 2 + 2048)[l]
             got_late = stage.tile([P, JH], U8, name=f"got_late{l}", align_bytes=64, offset=place)
             gather_scales(got_late[:], l, JH, JH)
             shift_scales(nc.sync, got_late[:], (J + l * JH) // 4)
+        quantize_wo(1)
+        for i in range(2, NT):
+            windows.append(stage.tile([P, T], F32, name=f"window{i}", align_bytes=64, offset=8192 * (i - 2)))
+            nc.gpsimd.memset(windows[i][:], 0.0)
         gate_sums(2)
         gate(2)
         for q in range(QUARTERS - 1):

@@ -82,8 +82,8 @@ def tile_list_rgg_ownsilu_kernel(
                 scales.bitcast(I32).rearrange("a q n -> q a n"),
             )
 
-        load_rows(0, wa_scales)
         nc.sync.dma_start(tab_w[:], tab_words[0].rearrange("p t b -> p (t b)").bitcast(I32))
+        load_rows(0, wa_scales)
         load_rows(1, wb_scales)
         load_rows(2, wc_scales)
         w_s8 = w_s[:].bitcast(U8)
@@ -210,7 +210,7 @@ def tile_list_rgg_ownsilu_kernel(
         result = [[keep.tile([P, JH], F32, name=f"result{i}{h}") for h in range(2)] for i in range(NT)]
 
         def gate_sums(k):
-            za = psum.tile([P, N], F32, name=f"za{k}", offset=2048 * (k % 2 if k % 2 or k <= 2 else 4))
+            za = psum.tile([P, N], F32, name=f"za{k}", offset=2048 * (4 if k in (3, 4, 6) else k % 2))
             ms = psum.tile([P, N], F32, name=f"ms{k}", offset=2048 * (2 + k % 2))
             product(za[:], [("a", DST), ("b", SRC)], k)
             product(ms[:], [("c", SRC)], k)
@@ -322,6 +322,8 @@ def tile_list_rgg_ownsilu_kernel(
                 own_half(1)
             for i in (0, 1):
                 scatter(i, q * JQ, JQ)
+            if 2 * q + 2 >= VECTOR_GATES:
+                gate(2 * q + 2)
             gate_sums(2 * q + 3)
             gate(2 * q + 3)
             turn(q, 1)
@@ -332,7 +334,8 @@ def tile_list_rgg_ownsilu_kernel(
                 own_sum(k)
             if 2 * q + 4 < BLOCKS:
                 gate_sums(2 * q + 4)
-                gate(2 * q + 4)
+                if 2 * q + 4 < VECTOR_GATES:
+                    gate(2 * q + 4)
         for pair in range(2):
             turn(QUARTERS - 1, pair)
         for i in range(NT - 1):

from contextlib import ExitStack

import concourse.mybir as mybir
from concourse.masks import make_identity

K, N, T, J = 1024, 512, 2048, 1024
FLOPS = 4 * 2 * K * N * J

F32 = mybir.dt.float32
BF16 = mybir.dt.bfloat16
I32 = mybir.dt.int32
U32 = mybir.dt.uint32
U16 = mybir.dt.uint16
U8 = mybir.dt.uint8
FP8X4 = mybir.dt.float8_e4m3fn_x4
FP4X4 = mybir.dt.float4_e2m1fn_x4
ACT = mybir.ActivationFunctionType
ALU = mybir.AluOpType

P = 128
PASSES = 2
JH = 512
NT = N // P
NH = 256
JQ = 2 * P
BLOCKS = J // P
QUARTERS = BLOCKS // 2
SHIFT_ROWS = 112
VECTOR_GATES = 5
SCALAR_ONES = (5, 6, 7)
GOT = 16384
GPSIMD_CLEARS = 1472
RAW = 32768
SUM_BANKS = 5
TURN_BANKS = 3


def tile_list_rgg_ownsilu_kernel(
    tc, tab_words, tab_scales, wa_words, wa_scales, wb_words, wb_scales, wc_words, wc_scales, wo, b, wgo, offs, offs2, out
):
    nc = tc.nc
    with ExitStack() as ctx:
        keep = ctx.enter_context(tc.tile_pool(name="keep", bufs=1))
        stage = ctx.enter_context(tc.tile_pool(name="stage", bufs=1))
        psum = ctx.enter_context(tc.psum_pool(name="psum", bufs=1))

        src_list = keep.tile([P, J // 16], U16, name="src_list")
        dst_list = keep.tile([P, J // 16], U16, name="dst_list")
        lists = (dst_list, src_list)
        DST, SRC = 0, 1

        tab_w = keep.tile([P, T], I32, name="tab_w", align_bytes=64)
        tab_s = keep.tile([P, T // 4], I32, name="tab_s", align_bytes=64)
        w_s = keep.tile([P, 3 * PASSES * N // 4], I32, name="w_s", align_bytes=64)
        shifted = keep.tile([P, 2 * J // 4], I32, name="shifted", align_bytes=64)
        windows = [keep.tile([P, T], F32, name=f"window{i}", align_bytes=64) for i in range(2)]
        warm = keep.tile([P, 1], F32, name="warm")

        nc.gpsimd.memset(tab_s[:], 0)
        nc.gpsimd.memset(w_s[:], 0)
        identity = keep.tile([P, P], F32, name="identity")
        make_identity(nc, identity[:])
        nc.gpsimd.memset(windows[0][:, 0:GPSIMD_CLEARS], 0.0)
        nc.vector.memset(warm[:], 0.0)
        for tile, first, last in ((shifted, 0, 2 * J // 4), (windows[1], 0, T), (windows[0], GPSIMD_CLEARS, T)):
            middle = (first + last) // 2 - 1
            nc.vector.memset(tile[:, first:middle], 0)
            nc.vector.memset(tile[:, middle:last], 0)
        nc.scalar.activation(warm[:], warm[:], ACT.Silu)

        nc.sync.dma_start(dst_list[:], offs2)
        for r in range(4):
            nc.sync.dma_start(
                tab_s[r:P:16, :], tab_scales.bitcast(I32).rearrange("a (q r) t -> r q a t", r=4)[r]
            )
        nc.sync.dma_start(src_list[:], offs)
        row_words = PASSES * N // 4

        def load_rows(w, scales):
            nc.sync.dma_start(
                w_s[0:P:8, w * row_words : (w + 1) * row_words].rearrange("q (a n) -> q a n", a=PASSES),
                scales.bitcast(I32).rearrange("a q n -> q a n"),
            )

        nc.sync.dma_start(tab_w[:], tab_words[0].rearrange("p t b -> p (t b)").bitcast(I32))
        load_rows(0, wa_scales)
        load_rows(1, wb_scales)
        load_rows(2, wc_scales)
        w_s8 = w_s[:].bitcast(U8)

        wo_raw = [
            [
                stage.tile([P, 4, NH], F32, name=f"wo_raw{a}{g}", align_bytes=64, offset=RAW + 4096 * (2 * a + g))[:]
                for g in range(2)
            ]
            for a in range(PASSES)
        ]

        def load_wo(a, g):
            rows = wo[512 * a : 512 * (a + 1), g * NH : (g + 1) * NH]
            nc.sync.dma_start(wo_raw[a][g], rows.rearrange("(p i) n -> p i n", i=4))

        wa_w = keep.tile([P, PASSES, N], I32, name="wa_w", align_bytes=64)
        wb_w = keep.tile([P, PASSES, N // 2], I32, name="wb_w", align_bytes=64)
        wc_w = keep.tile([P, PASSES, N // 2], I32, name="wc_w", align_bytes=64)
        edge_all = keep.tile([P, J], F32, name="edge_all")
        bias = keep.tile([P, NT], F32, name="bias")
        nc.sync.dma_start(wa_w[:], wa_words.rearrange("a p n i -> p a (n i)").bitcast(I32))
        nc.sync.dma_start(wb_w[:], wb_words.rearrange("a p x -> p a x").bitcast(I32))
        nc.sync.dma_start(wc_w[:], wc_words.rearrange("a p x -> p a x").bitcast(I32))
        for r in range(1, 4):
            nc.sync.dma_start(w_s[r:P:32, :], w_s[8 * r : P : 32, :])
        load_wo(0, 0)

        wo_w = keep.tile([P, PASSES, N], U32, name="wo_w", align_bytes=64)
        wo_s = keep.tile([P, PASSES, N], U8, name="wo_s", align_bytes=64)

        def quantize_wo(g):
            places = ((6144, 8192), (0, 7168))[g]
            wo_bf = [
                stage.tile([P, NH * 4], BF16, name=f"wo_bf{a}{g}", align_bytes=64, offset=places[a])
                for a in range(PASSES)
            ]
            for a in range(PASSES):
                first = 0
                if (a, g) == (1, 1):
                    first = NH // 2
                    nc.gpsimd.tensor_scalar(
                        wo_bf[a][:, 0 : 4 * first].rearrange("p (n i) -> p n i", i=4),
                        wo_raw[a][g][:, :, 0:first].rearrange("p i n -> p n i"),
                        1.0, 0.0, ALU.mult, ALU.add,
                    )
                nc.scalar.activation(
                    wo_bf[a][:, 4 * first :].rearrange("p (c e i) -> p c i e", e=4, i=4),
                    wo_raw[a][g][:, :, first:].rearrange("p i (c e) -> p c i e", e=4),
                    ACT.Copy,
                )
            for a in range(PASSES):
                nc.vector.quantize_mx(
                    out=wo_w[:, a, g * NH : (g + 1) * NH].bitcast(FP8X4),
                    scales=wo_s[:, a, g * NH : (g + 1) * NH],
                    in_=wo_bf[a][:],
                )

        got_early = keep.tile([P, 2 * JH], U8, name="got_early", align_bytes=64)
        parted = {}
        planes = {}

        def gather_scales(target, l, first, count):
            picks = lists[l][:, first // 16 : (first + count) // 16]
            nc.vector.tensor_copy(target, tab_s[:].bitcast(U8).indirect(picks))
            for at in range(0, count, P):
                planes[l, (first + at) // P, 0] = target[:, at : at + P]

        def shift_scales(queue, source, first):
            words = source.bitcast(I32)
            queue.dma_start(shifted[0:SHIFT_ROWS, first : first + words.shape[1]], words[16:P, :])

        for block in range(BLOCKS):
            for l in range(2):
                word = (block * P // JH * J + l * JH + block * P % JH) // 4
                planes[l, block, 1] = shifted[:, word : word + P // 4].bitcast(U8)

        def gather_words(first, count, places):
            got_w = [
                stage.tile([P, count], U32, name=f"got_w{first}_{l}", align_bytes=64, offset=places[l])
                for l in range(2)
            ]
            for l in range(2):
                picks = lists[l][:, first // 16 : (first + count) // 16]
                nc.vector.tensor_copy(got_w[l][:], tab_w[:].bitcast(U32).indirect(picks))
            return got_w

        def part_words(got_w, origin, first, count, places=None):
            for l in range(2):
                shape, name = [P, PASSES, 2 * count], f"parted{first}_{l}"
                if places is None:
                    codes = keep.tile(shape, U8, name=name, align_bytes=64)
                else:
                    codes = stage.tile(shape, U8, name=name, align_bytes=64, offset=places[l])
                words = got_w[l][:, first - origin : first - origin + count]
                nc.vector.tensor_copy(
                    codes[:].bitcast(U16), words.bitcast(U16).rearrange("p (j d) -> p d j", d=PASSES)
                )
                for at in range(0, count, P):
                    parted[l, (first + at) // P] = codes[:, :, 2 * at : 2 * (at + P)]

        def weight_operand(name, a, columns):
            if name == "o":
                return wo_w[:, a, columns].bitcast(FP8X4), wo_s[:, a, columns]
            first = ("abc".index(name) * PASSES + a) * N
            scales = w_s8[:, first : first + N]
            if name == "a":
                return wa_w[:, a, :].bitcast(FP8X4), scales
            words = wb_w if name == "b" else wc_w
            return words[:, a, :].bitcast(FP4X4), scales

        def product(acc, terms, block, columns=slice(0, N)):
            order = (0, 1) if block < 2 and terms[0][0] != "o" else (1, 0)
            passes = [(name, l, a) for a in order for name, l in terms]
            for s, (name, l, a) in enumerate(passes):
                w_codes, w_scales = weight_operand(name, a, columns)
                nc.tensor.matmul_mx(
                    out=acc, lhsT=parted[l, block][:, a, :].bitcast(FP4X4), lhsT_scale=planes[l, block, a],
                    rhs=w_codes, rhs_scale=w_scales, start=(s == 0), stop=(s == len(passes) - 1),
                )

        addends = {k: [] for k in range(BLOCKS)}
        factors = {}
        result = [[keep.tile([P, JH], F32, name=f"result{i}{h}") for h in range(2)] for i in range(NT)]

        def gate_sums(k):
            za = psum.tile([P, N], F32, name=f"za{k}", offset=2048 * (4 if k in (3, 4, 6) else k % 2))
            ms = psum.tile([P, N], F32, name=f"ms{k}", offset=2048 * (2 + k % 2))
            product(za[:], [("a", DST), ("b", SRC)], k)
            product(ms[:], [("c", SRC)], k)
            if k < 2:
                th = stage.tile([P, N], F32, name=f"th{k}", align_bytes=64, offset=RAW + 4096 * 2 + 2048 * k)
            else:
                th = keep.tile([P, N], F32, name=f"th{k}")
            nc.scalar.activation(th[:], za[:], ACT.Tanh, scale=0.5)
            if k < VECTOR_GATES:
                factors[k] = (th, ms)
            else:
                message = keep.tile([P, N], F32, name=f"message{k}")
                nc.scalar.activation(message[:], ms[:], ACT.Copy)
                factors[k] = (th, message)
                if k in SCALAR_ONES:
                    nc.scalar.activation(th[:], th[:], ACT.Copy, bias=1.0)
                else:
                    addends[k].append(message[:])

        def gate(k):
            gated = keep.tile([P, N], F32, name=f"gated{k}")
            th, message = factors[k]
            if k < VECTOR_GATES:
                nc.vector.scalar_tensor_tensor(gated[:], th[:], 1.0, message[:], ALU.add, ALU.mult)
            else:
                nc.gpsimd.tensor_tensor(gated[:], th[:], message[:], ALU.mult)
            addends[k].append(gated[:])

        def own_sum(k):
            ow = psum.tile([P, N], F32, name=f"ow{k}", offset=2048 * (k % 2))
            product(ow[:], [("o", DST)], k)
            own = keep.tile([P, N], F32, name=f"own{k}")
            addends[k].insert(0, own[:])
            nc.scalar.activation(own[:], ow[:], ACT.Copy, scale=2.0)

        own_first = keep.tile([P, 2, N], F32, name="own_first")
        for k in range(2):
            addends[k].append(own_first[:, k, :])

        def own_half(g):
            ow = psum.tile([P, 2, NH], F32, name=f"ow_first{g}", offset=2048 * (1 - g))
            for k in range(2):
                for c in range(NH // P):
                    product(ow[:, k, c * P : (c + 1) * P], [("o", DST)], k, slice(g * NH + c * P, g * NH + (c + 1) * P))
            nc.scalar.activation(own_first[:, :, g * NH : (g + 1) * NH], ow[:], ACT.Copy, scale=2.0)

        def turn(q, pair):
            h, first = divmod(q * JQ, JH)
            for i in (2 * pair, 2 * pair + 1):
                summed = psum.tile(
                    [P, 2, P], F32, name=f"summed{q}{i}", offset=2048 * (SUM_BANKS + (NT * q + i) % TURN_BANKS)
                )
                for j in range(2):
                    terms = addends[2 * q + j]
                    for s, term in enumerate(terms):
                        nc.tensor.matmul(
                            summed[:, j, :], lhsT=term[:, i * P : (i + 1) * P], rhs=identity[:],
                            is_transpose=True, start=(s == 0), stop=(s == len(terms) - 1),
                        )
                nc.scalar.activation(
                    result[i][h][:, first : first + JQ], summed[:].rearrange("p j t -> p (j t)"),
                    ACT.Silu, bias=bias[:, i : i + 1], scale=0.5,
                )

        def scatter(i, first, count):
            h, at = divmod(first, JH)
            values = result[i][h][:, at : at + count]
            places = windows[i][:].indirect(dst_list[:, first // 16 : (first + count) // 16])
            if first == 0 or first + count == J:
                nc.vector.tensor_tensor(places, values, edge_all[:, first : first + count], ALU.mult)
            else:
                nc.gpsimd.tensor_tensor(values, values, edge_all[:, first : first + count], ALU.mult)
                nc.vector.tensor_copy(places, values)
            if first + count == J:
                nc.sync.dma_start(out[i * P : (i + 1) * P, :], windows[i][:])

        for l in range(2):
            gather_scales(got_early[:, l * JH : (l + 1) * JH], l, 0, JH)
        shift_scales(nc.sync, got_early[:], 0)
        load_wo(1, 0)
        load_wo(0, 1)
        load_wo(1, 1)
        with nc.allow_non_contiguous_dma(reason="one bias value for each partition and row tile"):
            nc.sync.dma_start(bias[:], b.rearrange("(c p) -> p c", p=P))
        nc.sync.dma_start(edge_all[:], wgo)
        part_words(gather_words(0, JQ, (GOT + 2560, GOT + 6144)), 0, 0, JQ)
        rest = gather_words(JQ, J - JQ, (GOT, GOT + 3072))
        part_words(rest, JQ, JQ, JQ)
        part_words(rest, JQ, JH, JH)
        quantize_wo(0)
        for k in range(2):
            gate_sums(k)
            gate(k)
        own_half(0)
        for l in range(2):
            place = (GOT, RAW + 4096 * 2 + 2048)[l]
            got_late = stage.tile([P, JH], U8, name=f"got_late{l}", align_bytes=64, offset=place)
            gather_scales(got_late[:], l, JH, JH)
            shift_scales(nc.sync, got_late[:], (J + l * JH) // 4)
        quantize_wo(1)
        for i in range(2, NT):
            windows.append(stage.tile([P, T], F32, name=f"window{i}", align_bytes=64, offset=8192 * (i - 2)))
            nc.gpsimd.memset(windows[i][:], 0.0)
        gate_sums(2)
        gate(2)
        for q in range(QUARTERS - 1):
            turn(q, 0)
            if q == 0:
                own_half(1)
            for i in (0, 1):
                scatter(i, q * JQ, JQ)
            if 2 * q + 2 >= VECTOR_GATES:
                gate(2 * q + 2)
            gate_sums(2 * q + 3)
            gate(2 * q + 3)
            turn(q, 1)
            for i in (2, 3):
                if (q, i) != (QUARTERS - 2, NT - 1):
                    scatter(i, q * JQ, JQ)
            for k in (2 * q + 2, 2 * q + 3):
                own_sum(k)
            if 2 * q + 4 < BLOCKS:
                gate_sums(2 * q + 4)
                if 2 * q + 4 < VECTOR_GATES:
                    gate(2 * q + 4)
        for pair in range(2):
            turn(QUARTERS - 1, pair)
        for i in range(NT - 1):
            scatter(i, J - JQ, JQ)
        scatter(NT - 1, J - JH, JH)
